import numpy as np
import ml_dtypes


def mxq(x, axis, fmt="e4m3"):
    dtype, down = {"e4m3": (ml_dtypes.float8_e4m3fn, 7), "e5m2": (ml_dtypes.float8_e5m2, 14)}[fmt]
    v = np.moveaxis(np.asarray(x, np.float32).astype(ml_dtypes.bfloat16).astype(np.float64), axis, -1)
    blocks = v.reshape(v.shape[:-1] + (-1, 32))
    amax = np.abs(blocks).max(-1, keepdims=True)
    byte = np.maximum(np.where(amax > 0, np.frexp(amax)[1] - 1 + 127, 0) - down, 1)
    scale = np.exp2(byte - 127.0)
    codes = (blocks / scale).astype(np.float32).astype(dtype).astype(np.float64)
    return np.moveaxis((codes * scale).reshape(v.shape), -1, axis)


WIDE = False


def mx_kscale(k):
    if not WIDE:
        return np.ones(k)
    levels = np.array([10, -10, 5, -5, 0])
    if k % 512:
        return np.exp2(np.random.permutation(np.resize(levels, k // 32))).repeat(32)
    a = np.empty((k // 512, 16))
    for p in range(k // 512):
        a[p, :8] = np.random.permutation(np.resize(levels, 8))
        for g in range(8):
            far = levels[np.abs(levels - a[p, g]) >= 10]
            a[p, g + 8] = far[np.random.randint(len(far))]
    return np.exp2(a.ravel()).repeat(32)


def f64(x):
    return np.asarray(x).astype(np.float64)


def striped(idx):
    return np.tile(idx.reshape(-1, 16).T, (8, 1)).astype(np.uint16)


def unstriped(offs):
    return offs[:16].T.reshape(-1).astype(np.int64)


E2M1 = np.array([0.0, 0.5, 1.0, 1.5, 2.0, 3.0, 4.0, 6.0, -0.0, -0.5, -1.0, -1.5, -2.0, -3.0, -4.0, -6.0])


def pack_weight(w, fmt):
    k, n = w.shape
    w = f64(np.asarray(w, np.float32).astype(ml_dtypes.bfloat16)).reshape(k // 32, 32, n)
    amax = np.abs(w).max(1)
    if fmt == "e4m3":
        byte = np.frexp(amax)[1] - 1 + 127 - 7
    else:
        mant, ex = np.frexp(amax / 6.0)
        byte = np.where(mant > 0.5, ex, ex - 1) + 127
    byte = np.clip(np.where(amax > 0, byte, 1), 1, 254)
    scaled = (w * np.exp2(127.0 - byte)[:, None, :]).reshape(k, n).astype(np.float32)
    by_word = np.ascontiguousarray(scaled.reshape(k // 512, 128, 4, n).transpose(0, 1, 3, 2))
    if fmt == "e4m3":
        words = by_word.astype(ml_dtypes.float8_e4m3fn).view(np.uint8)
    else:
        c = by_word.astype(ml_dtypes.float4_e2m1fn).view(np.uint8) & 0xF
        words = (c[..., 0::2] | (c[..., 1::2] << 4)).reshape(k // 512, 128, 2 * n)
    return np.ascontiguousarray(words), np.ascontiguousarray(byte.astype(np.uint8).reshape(k // 512, 16, n))


def unpack_weight(words, scales, fmt):
    g, _, n = scales.shape
    words = np.ascontiguousarray(words).reshape(g, 128, n, -1)
    if fmt == "e4m3":
        vals = words.view(ml_dtypes.float8_e4m3fn).astype(np.float64)
    else:
        nib = np.empty((g, 128, n, 4), np.uint8)
        nib[..., 0::2] = words & 0xF
        nib[..., 1::2] = words >> 4
        vals = E2M1[nib]
    vals = vals * np.repeat(np.exp2(scales.astype(np.float64) - 127.0), 8, axis=1)[..., None]
    return vals.transpose(0, 1, 3, 2).reshape(g * 512, n)


def gelu(v):
    return 0.5 * v * (1.0 + np.tanh(np.sqrt(2.0 / np.pi) * (v + 0.044715 * v**3)))


def often(T, S):
    return np.random.permutation(T)[(T * np.random.uniform(0, 1, S) ** 4).astype(np.int64)]


K, T, S, H, T2, P, N = 1024, 2048, 1024, 1024, 1024, 512, 512

def setup_inputs():
    n = np.random.standard_normal
    s = mx_kscale(K)[:, None]
    u = mx_kscale(H)[:, None]
    tab_words, tab_scales = pack_weight(n((K, T)) * s, "e4m3")
    tab2_words, tab2_scales = pack_weight(n((K, T2)) * s, "e4m3")
    wa_words, wa_scales = pack_weight(0.6 * n((K, H)) / np.sqrt(K) / s, "e2m1")
    wb = (0.6 * n((K, H)) / np.sqrt(K) / s).astype(np.float32)
    wf_words, wf_scales = pack_weight(n((H, N)) / np.sqrt(H) / u, "e4m3")
    drive = (np.exp(0.3 * n(H)) * u[:, 0]).astype(np.float32)
    return {"tab_words": tab_words, "tab_scales": tab_scales,
            "tab2_words": tab2_words, "tab2_scales": tab2_scales,
            "wa_words": wa_words, "wa_scales": wa_scales, "wb": wb,
            "wf_words": wf_words, "wf_scales": wf_scales, "drive": drive,
            "offs": striped(np.random.permutation(T)[:S]),
            "pos1": striped(often(S, P)),
            "offs2": striped(np.random.permutation(T2)[:P])}

def reference(tab_words, tab_scales, tab2_words, tab2_scales, wa_words, wa_scales, wb,
              wf_words, wf_scales, drive, offs, pos1, offs2):
    v = unpack_weight(tab_words, tab_scales, "e4m3")[:, unstriped(offs)]
    v2 = unpack_weight(tab2_words, tab2_scales, "e4m3")[:, unstriped(offs2)]
    wa = unpack_weight(wa_words, wa_scales, "e2m1")
    wf = unpack_weight(wf_words, wf_scales, "e4m3")
    ra = np.exp(-(wa.T @ v))
    rb = np.exp(-(mxq(f64(wb), 0, "e4m3").T @ v2))
    series = ra[:, unstriped(pos1)] + rb
    z = f64(drive)[:, None] / series
    return wf.T @ mxq(z, 0, "e4m3")

@@ -1,0 +1,275 @@
+from contextlib import ExitStack
+
+import concourse.mybir as mybir
+
+K, T, S, H, T2, M, N = 1024, 2048, 1024, 1024, 1024, 512, 512
+FLOPS = 2 * K * H * S + 2 * K * H * M + 2 * H * N * M
+
+F32 = mybir.dt.float32
+BF16 = mybir.dt.bfloat16
+I32 = mybir.dt.int32
+U32 = mybir.dt.uint32
+U16 = mybir.dt.uint16
+U8 = mybir.dt.uint8
+FP8X4 = mybir.dt.float8_e4m3fn_x4
+FP4X4 = mybir.dt.float4_e2m1fn_x4
+ACT = mybir.ActivationFunctionType
+ALU = mybir.AluOpType
+
+P = 128
+PACK = 4
+KP = P * PACK
+BANK = 512
+HALF = M // 2
+
+
+def tile_list_airway_series_conductance_kernel(
+    tc, tab_words, tab_scales, tab2_words, tab2_scales, wa_words, wa_scales, wb,
+    wf_words, wf_scales, drive, offs, pos1, offs2, out,
+):
+    nc = tc.nc
+    with ExitStack() as ctx:
+        keep = ctx.enter_context(tc.tile_pool(name="keep", bufs=1))
+        psum = ctx.enter_context(tc.psum_pool(name="psum", bufs=1))
+
+        def sb(name, shape, dtype):
+            return keep.tile(shape, dtype, name=name, align_bytes=64)
+
+        offs_t = sb("offs_t", [P, S // 16], U16)
+        pos_t = sb("pos_t", [P, M // 16], U16)
+        offs2_t = sb("offs2_t", [P, M // 16], U16)
+
+        tab_s = sb("tab_s", [P, T], U8)
+        wa_s_raw = sb("wa_s_raw", [P, 2, H], U8)
+        tab2_s = sb("tab2_s", [P, T2], U8)
+        wf_s = sb("wf_s", [P, N], U8)
+        v_s1 = sb("v_s1", [P, S], U8)
+        nc.gpsimd.memset(tab_s[:].bitcast(I32), 0)
+        nc.vector.memset(wa_s_raw[:].rearrange("p a n -> p (a n)").bitcast(I32), 0)
+        for plane in (tab2_s, wf_s, v_s1):
+            nc.gpsimd.memset(plane[:].bitcast(I32), 0)
+        minus_one = keep.tile([P, 2 * PACK], F32, name="minus_one", tag="column")
+        nc.gpsimd.memset(minus_one[:], -1.0)
+
+        def load_side_by_side(plane, scales):
+            for q in range(4):
+                nc.scalar.dma_start(
+                    out=plane[32 * q : 32 * q + 4, :, :].bitcast(I32),
+                    in_=scales[:, 4 * q : 4 * q + 4, :].rearrange("a r n -> r a n").bitcast(I32),
+                )
+
+        def load_packed(plane, scales, queue):
+            for q in range(4):
+                queue.dma_start(
+                    out=plane[32 * q : 32 * q + 8, :].bitcast(I32),
+                    in_=scales[:, 4 * q : 4 * q + 4, :].bitcast(I32),
+                )
+
+        def load_words(name, words):
+            tile = sb(name, [P, words.shape[1]], I32)
+            nc.sync.dma_start(out=tile[:], in_=words.rearrange("p n i -> p (n i)").bitcast(I32))
+            return tile
+
+        def load_wb(a, b):
+            tile = sb("wb_raw%d%d" % (a, b), [P, PACK, KP], F32)
+            rows = wb[KP * a : KP * (a + 1), KP * b : KP * (b + 1)]
+            nc.sync.dma_start(out=tile[:], in_=rows.rearrange("(p j) c -> p j c", j=PACK))
+            return tile
+
+        wa_raw = sb("wa_raw", [P, 2, H // 2], I32)
+        nc.sync.dma_start(out=offs_t[:], in_=offs)
+        nc.sync.dma_start(out=wa_raw[:], in_=wa_words.rearrange("a p n -> p a n").bitcast(I32))
+        load_packed(tab_s, tab_scales, nc.scalar)
+        load_side_by_side(wa_s_raw, wa_scales)
+        load_packed(tab2_s, tab2_scales, nc.gpsimd)
+        wb_raw = {}
+        tab_w = [load_words("tab_w0", tab_words[0])]
+        wb_raw[0, 0] = load_wb(0, 0)
+        tab_w.append(load_words("tab_w1", tab_words[1]))
+        nc.sync.dma_start(out=offs2_t[:], in_=offs2)
+        tab2_w = [load_words("tab2_w%d" % a, tab2_words[a]) for a in range(2)]
+        for a, b in ((1, 0), (0, 1), (1, 1)):
+            wb_raw[a, b] = load_wb(a, b)
+        nc.sync.dma_start(out=pos_t[:], in_=pos1)
+        drive_t = sb("drive_t", [P, 2, PACK], F32)
+        nc.sync.dma_start(out=drive_t[:], in_=drive.rearrange("(b p t) -> p b t", p=P, t=PACK))
+        load_packed(wf_s, wf_scales, nc.sync)
+        wf_w = sb("wf_w", [P, 2, N], I32)
+        nc.sync.dma_start(
+            out=wf_w[:], in_=wf_words.rearrange("a p n i -> p a (n i)").bitcast(I32)
+        )
+
+        wa_w = sb("wa_w", [P, 2, 2 * H], U8)
+        nc.vector.tensor_copy(
+            out=wa_w[:].rearrange("p a n -> p (a n)").bitcast(U16).rearrange(
+                "p (g t c i) -> p g c t i", t=PACK, c=16, i=8),
+            in_=wa_raw[:].rearrange("p a n -> p (a n)").bitcast(U16).rearrange(
+                "p (g c i t) -> p g c t i", t=PACK, c=16, i=8),
+        )
+        v_s0 = sb("v_s0", [P, S], U8)
+        nc.vector.tensor_copy(out=v_s0[:], in_=tab_s[:].indirect(offs_t[:]))
+        nc.scalar.dma_start(out=v_s1[0:112, :].bitcast(I32), in_=v_s0[4:116, :].bitcast(I32))
+        wa_s = sb("wa_s", [P, 2, H], U8)
+        nc.vector.tensor_copy(
+            out=wa_s[:].rearrange("p a (b t c i) -> p (a b) c t i", t=PACK, c=8, i=16),
+            in_=wa_s_raw[:].rearrange("p a (b c i t) -> p (a b) c t i", t=PACK, c=8, i=16),
+        )
+        v_s = [v_s0, v_s1]
+
+        def gather(name, window, offsets, count, dtype, tag=""):
+            tile = keep.tile([P, count], dtype, name=name, align_bytes=64, tag=tag)
+            nc.vector.tensor_copy(out=tile[:], in_=window.indirect(offsets))
+            return tile
+
+        wb_bf = {}
+
+        def cast_wb(a, b, engine_copy, tag=""):
+            tile = keep.tile([P, KP * PACK], BF16, name="wb_bf%d%d" % (a, b), align_bytes=64, tag=tag)
+            engine_copy(
+                out=tile[:].rearrange("p (t m j) -> p m t j", t=PACK, j=PACK),
+                in_=wb_raw[a, b][:].rearrange("p j (m t) -> p m t j", t=PACK),
+            )
+            wb_bf[a, b] = tile
+
+        def quantize(name, src, words):
+            codes = sb(name + "_w", [P, words], U32)
+            scales = sb(name + "_s", [P, words], U8)
+            nc.vector.quantize_mx(out=codes[:].bitcast(FP8X4), scales=scales[:], in_=src)
+            return codes, scales
+
+        cast_wb(0, 0, nc.scalar.copy)
+        v_w = {}
+        for a in range(2):
+            for h in range(2):
+                v_w[a, h] = gather("v_w%d%d" % (a, h), tab_w[a][:].bitcast(U32),
+                                   offs_t[:, 32 * h : 32 * (h + 1)], BANK, U32)
+        v2_w = [gather("v2_w%d" % a, tab2_w[a][:].bitcast(U32), offs2_t[:], M, U32) for a in range(2)]
+        v2_s = gather("v2_s", tab2_s[:], offs2_t[:], M, U8)
+        wb_q = {}
+
+        ra, rb = {}, {}
+
+        def make_ra(b, t, h):
+            if h == 0:
+                ra[b, t] = sb("ra%d%d" % (b, t), [P, S], F32)
+            c0 = KP * b + P * t
+            cols = slice(BANK * h, BANK * (h + 1))
+            acc = psum.tile([P, BANK], F32, name="acc_a", bufs=4)
+            for a in range(2):
+                nc.tensor.matmul_mx(
+                    out=acc[:],
+                    lhsT=wa_w[:, a, 2 * c0 : 2 * (c0 + P)].bitcast(FP4X4),
+                    lhsT_scale=wa_s[:, a, c0 : c0 + P],
+                    rhs=v_w[a, h][:].bitcast(FP8X4),
+                    rhs_scale=v_s[a][:, cols],
+                    start=(a == 0), stop=(a == 1),
+                )
+            nc.scalar.activation(out=ra[b, t][:, cols], in_=acc[:], func=ACT.Exp, scale=minus_one[:, 0:1])
+
+        def make_rb(b, t):
+            tile = sb("rb%d%d" % (b, t), [P, M], F32)
+            cols = slice(P * t, P * (t + 1))
+            acc = psum.tile([P, BANK], F32, name="acc_b", bufs=2)
+            for a in range(2):
+                codes, scales = wb_q[a, b]
+                nc.tensor.matmul_mx(
+                    out=acc[:],
+                    lhsT=codes[:, cols].bitcast(FP8X4),
+                    lhsT_scale=scales[:, cols],
+                    rhs=v2_w[a][:].bitcast(FP8X4),
+                    rhs_scale=v2_s[4 * a : P, :],
+                    start=(a == 0), stop=(a == 1),
+                )
+            nc.scalar.activation(out=tile[:], in_=acc[:], func=ACT.Exp, scale=minus_one[:, 0:1])
+            rb[b, t] = tile
+
+        series = {}
+
+        def make_series(b, t, c0, width):
+            tag = "series%d%d" % (b if c0 == 0 else 0, t)
+            tile = keep.tile([P, width], F32, name="series%d%d_%d" % (b, t, c0), align_bytes=64, tag=tag)
+            nc.vector.tensor_tensor(
+                out=tile[:],
+                in0=ra[b, t][:].indirect(pos_t[:, c0 // 16 : (c0 + width) // 16]),
+                in1=rb[b, t][:, c0 : c0 + width],
+                op=ALU.add,
+            )
+            series[b, t, c0] = tile
+
+        def make_root(b, c0, width):
+            root = sb("root%d_%d" % (b, c0), [P, PACK, width], F32)
+            for t in range(PACK):
+                s = PACK * b + t
+                nc.scalar.activation(
+                    out=root[:, t, :], in_=series[b, t, c0][:],
+                    func=ACT.Abs_reciprocal_sqrt, scale=inv_drive[:, s : s + 1],
+                )
+            return root
+
+        def make_z(b, c0, width, root):
+            z_bf = sb("z_bf%d_%d" % (b, c0), [P, width * PACK], BF16)
+            dst = z_bf[:].rearrange("p (c i t) -> p c t i", i=4, t=PACK)
+            src = root[:].rearrange("p t (c i) -> p c t i", i=4)
+            if b == 1 and c0 == 0:
+                nc.vector.tensor_tensor(out=dst, in0=src, in1=src, op=ALU.mult)
+            else:
+                nc.scalar.activation(out=dst, in_=src, func=ACT.Square)
+            return quantize("z_q%d_%d" % (b, c0), z_bf[:], width)
+
+        for h in range(2):
+            for t in range(PACK):
+                make_ra(0, t, h)
+        cast_wb(1, 0, nc.vector.tensor_copy, tag="tab2_w0")
+        for a in range(2):
+            wb_q[a, 0] = quantize("wb_q%d0" % a, wb_bf[a, 0][:], KP)
+        cast_wb(0, 1, nc.vector.tensor_copy, tag="tab2_w1")
+        cast_wb(1, 1, nc.vector.tensor_copy, tag="tab2_w0")
+        for a in range(2):
+            wb_q[a, 1] = quantize("wb_q%d1" % a, wb_bf[a, 1][:], KP)
+        inv_early = sb("inv_early", [P, 2 * PACK], F32)
+        nc.vector.reciprocal(out=inv_early[:], in_=drive_t[:].rearrange("p b t -> p (b t)"))
+        for t in range(2):
+            for h in range(2):
+                make_ra(1, t, h)
+        for t in range(PACK):
+            make_rb(0, t)
+        for t in range(2, PACK):
+            for h in range(2):
+                make_ra(1, t, h)
+        for t in range(PACK):
+            make_series(0, t, 0, M)
+        for t in range(PACK):
+            make_rb(1, t)
+        inv_drive = keep.tile([P, 2 * PACK], F32, name="inv_drive", tag="column")
+        nc.scalar.copy(out=inv_drive[:], in_=inv_early[:])
+        for t in range(PACK):
+            make_series(1, t, 0, HALF)
+        root0 = make_root(0, 0, M)
+        for t in range(PACK):
+            make_series(1, t, HALF, HALF)
+        z0 = make_z(0, 0, M, root0)
+        root1 = [make_root(1, HALF * h, HALF) for h in range(2)]
+        for h in range(2):
+            z1 = make_z(1, HALF * h, HALF, root1[h])
+            mcols = slice(HALF * h, HALF * (h + 1))
+            for pair in range(2):
+                acc = psum.tile([P, 2, HALF], F32, name="acc_o", bufs=2)
+                for j in range(2):
+                    ncols = slice(P * (2 * pair + j), P * (2 * pair + j + 1))
+                    for b in range(2):
+                        codes, scales = (z0[0][:, mcols], z0[1][:, mcols]) if b == 0 else (z1[0][:], z1[1][:])
+                        nc.tensor.matmul_mx(
+                            out=acc[:, j, :],
+                            lhsT=wf_w[:, b, ncols].bitcast(FP8X4),
+                            lhsT_scale=wf_s[4 * b : P, ncols],
+                            rhs=codes.bitcast(FP8X4),
+                            rhs_scale=scales,
+                            start=(b == 0), stop=(b == 1),
+                        )
+                res = sb("res%d%d" % (h, pair), [P, 2, HALF], F32)
+                if pair == 0:
+                    nc.vector.tensor_copy(out=res[:], in_=acc[:])
+                else:
+                    nc.scalar.copy(out=res[:], in_=acc[:])
+                rows = out[2 * P * pair : 2 * P * (pair + 1), mcols]
+                nc.sync.dma_start(out=rows.rearrange("(j p) m -> p j m", p=P), in_=res[:])

@@ -53,7 +53,7 @@ def tile_list_airway_series_conductance_kernel(
 
         def load_side_by_side(plane, scales):
             for q in range(4):
-                nc.scalar.dma_start(
+                nc.sync.dma_start(
                     out=plane[32 * q : 32 * q + 4, :, :].bitcast(I32),
                     in_=scales[:, 4 * q : 4 * q + 4, :].rearrange("a r n -> r a n").bitcast(I32),
                 )
@@ -79,15 +79,15 @@ def tile_list_airway_series_conductance_kernel(
         wa_raw = sb("wa_raw", [P, 2, H // 2], I32)
         nc.sync.dma_start(out=offs_t[:], in_=offs)
         nc.sync.dma_start(out=wa_raw[:], in_=wa_words.rearrange("a p n -> p a n").bitcast(I32))
-        load_packed(tab_s, tab_scales, nc.scalar)
-        load_side_by_side(wa_s_raw, wa_scales)
-        load_packed(tab2_s, tab2_scales, nc.gpsimd)
+        load_packed(tab_s, tab_scales, nc.sync)
         wb_raw = {}
         tab_w = [load_words("tab_w0", tab_words[0])]
         wb_raw[0, 0] = load_wb(0, 0)
+        load_side_by_side(wa_s_raw, wa_scales)
         tab_w.append(load_words("tab_w1", tab_words[1]))
-        nc.sync.dma_start(out=offs2_t[:], in_=offs2)
         tab2_w = [load_words("tab2_w%d" % a, tab2_words[a]) for a in range(2)]
+        nc.sync.dma_start(out=offs2_t[:], in_=offs2)
+        load_packed(tab2_s, tab2_scales, nc.sync)
         for a, b in ((1, 0), (0, 1), (1, 1)):
             wb_raw[a, b] = load_wb(a, b)
         nc.sync.dma_start(out=pos_t[:], in_=pos1)
@@ -108,12 +108,7 @@ def tile_list_airway_series_conductance_kernel(
         )
         v_s0 = sb("v_s0", [P, S], U8)
         nc.vector.tensor_copy(out=v_s0[:], in_=tab_s[:].indirect(offs_t[:]))
-        nc.scalar.dma_start(out=v_s1[0:112, :].bitcast(I32), in_=v_s0[4:116, :].bitcast(I32))
-        wa_s = sb("wa_s", [P, 2, H], U8)
-        nc.vector.tensor_copy(
-            out=wa_s[:].rearrange("p a (b t c i) -> p (a b) c t i", t=PACK, c=8, i=16),
-            in_=wa_s_raw[:].rearrange("p a (b c i t) -> p (a b) c t i", t=PACK, c=8, i=16),
-        )
+        nc.gpsimd.dma_start(out=v_s1[0:112, :].bitcast(I32), in_=v_s0[4:116, :].bitcast(I32))
         v_s = [v_s0, v_s1]
 
         def gather(name, window, offsets, count, dtype, tag=""):
@@ -139,10 +134,19 @@ def tile_list_airway_series_conductance_kernel(
 
         cast_wb(0, 0, nc.scalar.copy)
         v_w = {}
-        for a in range(2):
+
+        def gather_pass(a):
             for h in range(2):
                 v_w[a, h] = gather("v_w%d%d" % (a, h), tab_w[a][:].bitcast(U32),
                                    offs_t[:, 32 * h : 32 * (h + 1)], BANK, U32)
+
+        gather_pass(0)
+        wa_s = keep.tile([P, 2, H], U8, name="wa_s", align_bytes=64, tag="tab_w0")
+        nc.vector.tensor_copy(
+            out=wa_s[:].rearrange("p a (b t c i) -> p (a b) c t i", t=PACK, c=8, i=16),
+            in_=wa_s_raw[:].rearrange("p a (b c i t) -> p (a b) c t i", t=PACK, c=8, i=16),
+        )
+        gather_pass(1)
         v2_w = [gather("v2_w%d" % a, tab2_w[a][:].bitcast(U32), offs2_t[:], M, U32) for a in range(2)]
         v2_s = gather("v2_s", tab2_s[:], offs2_t[:], M, U8)
         wb_q = {}
@@ -154,7 +158,7 @@ def tile_list_airway_series_conductance_kernel(
                 ra[b, t] = sb("ra%d%d" % (b, t), [P, S], F32)
             c0 = KP * b + P * t
             cols = slice(BANK * h, BANK * (h + 1))
-            acc = psum.tile([P, BANK], F32, name="acc_a", bufs=4)
+            acc = psum.tile([P, BANK], F32, name="acc", bufs=8)
             for a in range(2):
                 nc.tensor.matmul_mx(
                     out=acc[:],
@@ -169,7 +173,7 @@ def tile_list_airway_series_conductance_kernel(
         def make_rb(b, t):
             tile = sb("rb%d%d" % (b, t), [P, M], F32)
             cols = slice(P * t, P * (t + 1))
-            acc = psum.tile([P, BANK], F32, name="acc_b", bufs=2)
+            acc = psum.tile([P, BANK], F32, name="acc", bufs=8)
             for a in range(2):
                 codes, scales = wb_q[a, b]
                 nc.tensor.matmul_mx(
@@ -183,38 +187,36 @@ def tile_list_airway_series_conductance_kernel(
             nc.scalar.activation(out=tile[:], in_=acc[:], func=ACT.Exp, scale=minus_one[:, 0:1])
             rb[b, t] = tile
 
-        series = {}
+        def make_series(b, c0, width, tag):
+            tile = keep.tile([P, PACK, width], F32, name="series%d_%d" % (b, c0), align_bytes=64, tag=tag)
+            for t in range(PACK):
+                nc.vector.tensor_tensor(
+                    out=tile[:, t, :],
+                    in0=ra[b, t][:].indirect(pos_t[:, c0 // 16 : (c0 + width) // 16]),
+                    in1=rb[b, t][:, c0 : c0 + width],
+                    op=ALU.add,
+                )
+            return tile
 
-        def make_series(b, t, c0, width):
-            tag = "series%d%d" % (b if c0 == 0 else 0, t)
-            tile = keep.tile([P, width], F32, name="series%d%d_%d" % (b, t, c0), align_bytes=64, tag=tag)
-            nc.vector.tensor_tensor(
-                out=tile[:],
-                in0=ra[b, t][:].indirect(pos_t[:, c0 // 16 : (c0 + width) // 16]),
-                in1=rb[b, t][:, c0 : c0 + width],
-                op=ALU.add,
-            )
-            series[b, t, c0] = tile
-
-        def make_root(b, c0, width):
-            root = sb("root%d_%d" % (b, c0), [P, PACK, width], F32)
+        def make_root(b, h, series):
+            root = sb("root%d%d" % (b, h), [P, PACK, HALF], F32)
             for t in range(PACK):
                 s = PACK * b + t
                 nc.scalar.activation(
-                    out=root[:, t, :], in_=series[b, t, c0][:],
+                    out=root[:, t, :], in_=series[:, t, :],
                     func=ACT.Abs_reciprocal_sqrt, scale=inv_drive[:, s : s + 1],
                 )
             return root
 
-        def make_z(b, c0, width, root):
-            z_bf = sb("z_bf%d_%d" % (b, c0), [P, width * PACK], BF16)
+        def make_z(b, h, root, on_vector):
+            z_bf = sb("z_bf%d%d" % (b, h), [P, HALF * PACK], BF16)
             dst = z_bf[:].rearrange("p (c i t) -> p c t i", i=4, t=PACK)
             src = root[:].rearrange("p t (c i) -> p c t i", i=4)
-            if b == 1 and c0 == 0:
+            if on_vector:
                 nc.vector.tensor_tensor(out=dst, in0=src, in1=src, op=ALU.mult)
             else:
                 nc.scalar.activation(out=dst, in_=src, func=ACT.Square)
-            return quantize("z_q%d_%d" % (b, c0), z_bf[:], width)
+            return quantize("z_q%d%d" % (b, h), z_bf[:], HALF)
 
         for h in range(2):
             for t in range(PACK):
@@ -236,40 +238,37 @@ def tile_list_airway_series_conductance_kernel(
         for t in range(2, PACK):
             for h in range(2):
                 make_ra(1, t, h)
-        for t in range(PACK):
-            make_series(0, t, 0, M)
+        series0 = make_series(0, 0, M, "tab2_w0")
         for t in range(PACK):
             make_rb(1, t)
         inv_drive = keep.tile([P, 2 * PACK], F32, name="inv_drive", tag="column")
         nc.scalar.copy(out=inv_drive[:], in_=inv_early[:])
-        for t in range(PACK):
-            make_series(1, t, 0, HALF)
-        root0 = make_root(0, 0, M)
-        for t in range(PACK):
-            make_series(1, t, HALF, HALF)
-        z0 = make_z(0, 0, M, root0)
-        root1 = [make_root(1, HALF * h, HALF) for h in range(2)]
+        series = {(0, h): series0[:, :, HALF * h : HALF * (h + 1)] for h in range(2)}
+        series[1, 0] = make_series(1, 0, HALF, "series1")
+        series[1, 1] = make_series(1, HALF, HALF, "wb_q11_w")
+        results = []
+
         for h in range(2):
-            z1 = make_z(1, HALF * h, HALF, root1[h])
             mcols = slice(HALF * h, HALF * (h + 1))
+            accs = [psum.tile([P, BANK], F32, name="acc", bufs=8) for j in range(4)]
+            for b in range(2):
+                codes, scales = make_z(b, h, make_root(b, h, series[b, h]), on_vector=(b != h))
+                for j in range(4):
+                    ncols = slice(P * j, P * (j + 1))
+                    nc.tensor.matmul_mx(
+                        out=accs[j][:, 0:HALF],
+                        lhsT=wf_w[:, b, ncols].bitcast(FP8X4),
+                        lhsT_scale=wf_s[4 * b : P, ncols],
+                        rhs=codes[:].bitcast(FP8X4),
+                        rhs_scale=scales[:],
+                        start=(b == 0), stop=(b == 1),
+                    )
+            results.append((accs, mcols))
+        for h, (accs, mcols) in enumerate(results):
             for pair in range(2):
-                acc = psum.tile([P, 2, HALF], F32, name="acc_o", bufs=2)
-                for j in range(2):
-                    ncols = slice(P * (2 * pair + j), P * (2 * pair + j + 1))
-                    for b in range(2):
-                        codes, scales = (z0[0][:, mcols], z0[1][:, mcols]) if b == 0 else (z1[0][:], z1[1][:])
-                        nc.tensor.matmul_mx(
-                            out=acc[:, j, :],
-                            lhsT=wf_w[:, b, ncols].bitcast(FP8X4),
-                            lhsT_scale=wf_s[4 * b : P, ncols],
-                            rhs=codes.bitcast(FP8X4),
-                            rhs_scale=scales,
-                            start=(b == 0), stop=(b == 1),
-                        )
                 res = sb("res%d%d" % (h, pair), [P, 2, HALF], F32)
-                if pair == 0:
-                    nc.vector.tensor_copy(out=res[:], in_=acc[:])
-                else:
-                    nc.scalar.copy(out=res[:], in_=acc[:])
+                copies = (nc.scalar.copy if h == 0 else nc.vector.tensor_copy, nc.scalar.copy)
+                for i, engine_copy in enumerate(copies):
+                    engine_copy(out=res[:, i, :], in_=accs[2 * pair + i][:, 0:HALF])
                 rows = out[2 * P * pair : 2 * P * (pair + 1), mcols]
                 nc.sync.dma_start(out=rows.rearrange("(j p) m -> p j m", p=P), in_=res[:])

@@ -44,8 +44,8 @@ def tile_list_airway_series_conductance_kernel(
         tab2_s = sb("tab2_s", [P, T2], U8)
         wf_s = sb("wf_s", [P, N], U8)
         v_s1 = sb("v_s1", [P, S], U8)
-        nc.gpsimd.memset(tab_s[:].bitcast(I32), 0)
-        nc.vector.memset(wa_s_raw[:].rearrange("p a n -> p (a n)").bitcast(I32), 0)
+        nc.vector.memset(tab_s[:].bitcast(I32), 0)
+        nc.gpsimd.memset(wa_s_raw[:].rearrange("p a n -> p (a n)").bitcast(I32), 0)
         for plane in (tab2_s, wf_s, v_s1):
             nc.gpsimd.memset(plane[:].bitcast(I32), 0)
         minus_one = keep.tile([P, 2 * PACK], F32, name="minus_one", tag="column")
@@ -78,8 +78,8 @@ def tile_list_airway_series_conductance_kernel(
 
         wa_raw = sb("wa_raw", [P, 2, H // 2], I32)
         nc.sync.dma_start(out=offs_t[:], in_=offs)
-        nc.sync.dma_start(out=wa_raw[:], in_=wa_words.rearrange("a p n -> p a n").bitcast(I32))
         load_packed(tab_s, tab_scales, nc.sync)
+        nc.sync.dma_start(out=wa_raw[:], in_=wa_words.rearrange("a p n -> p a n").bitcast(I32))
         wb_raw = {}
         tab_w = [load_words("tab_w0", tab_words[0])]
         wb_raw[0, 0] = load_wb(0, 0)
@@ -99,6 +99,11 @@ def tile_list_airway_series_conductance_kernel(
             out=wf_w[:], in_=wf_words.rearrange("a p n i -> p a (n i)").bitcast(I32)
         )
 
+        v_s0 = sb("v_s0", [P, S], U8)
+        nc.vector.tensor_copy(out=v_s0[:], in_=tab_s[:].indirect(offs_t[:]))
+        nc.gpsimd.dma_start(out=v_s1[0:112, :].bitcast(I32), in_=v_s0[4:116, :].bitcast(I32))
+        v_s = [v_s0, v_s1]
+
         wa_w = sb("wa_w", [P, 2, 2 * H], U8)
         nc.vector.tensor_copy(
             out=wa_w[:].rearrange("p a n -> p (a n)").bitcast(U16).rearrange(
@@ -106,10 +111,6 @@ def tile_list_airway_series_conductance_kernel(
             in_=wa_raw[:].rearrange("p a n -> p (a n)").bitcast(U16).rearrange(
                 "p (g c i t) -> p g c t i", t=PACK, c=16, i=8),
         )
-        v_s0 = sb("v_s0", [P, S], U8)
-        nc.vector.tensor_copy(out=v_s0[:], in_=tab_s[:].indirect(offs_t[:]))
-        nc.gpsimd.dma_start(out=v_s1[0:112, :].bitcast(I32), in_=v_s0[4:116, :].bitcast(I32))
-        v_s = [v_s0, v_s1]
 
         def gather(name, window, offsets, count, dtype, tag=""):
             tile = keep.tile([P, count], dtype, name=name, align_bytes=64, tag=tag)
@@ -168,7 +169,7 @@ def tile_list_airway_series_conductance_kernel(
                     rhs_scale=v_s[a][:, cols],
                     start=(a == 0), stop=(a == 1),
                 )
-            nc.scalar.activation(out=ra[b, t][:, cols], in_=acc[:], func=ACT.Exp, scale=minus_one[:, 0:1])
+            nc.scalar.activation(out=ra[b, t][:, cols], in_=acc[:], func=ACT.Exp, scale=-1.0)
 
         def make_rb(b, t):
             tile = sb("rb%d%d" % (b, t), [P, M], F32)
@@ -184,7 +185,8 @@ def tile_list_airway_series_conductance_kernel(
                     rhs_scale=v2_s[4 * a : P, :],
                     start=(a == 0), stop=(a == 1),
                 )
-            nc.scalar.activation(out=tile[:], in_=acc[:], func=ACT.Exp, scale=minus_one[:, 0:1])
+            scale = minus_one[:, 0:1] if b == 1 else -1.0
+            nc.scalar.activation(out=tile[:], in_=acc[:], func=ACT.Exp, scale=scale)
             rb[b, t] = tile
 
         def make_series(b, c0, width, tag):

@@ -20,7 +20,8 @@ P = 128
 PACK = 4
 KP = P * PACK
 BANK = 512
-HALF = M // 2
+PLACES = {"dealt": 0}
+CHUNKS = ((0, 256), (256, 128), (384, 128))
 
 
 def tile_list_airway_series_conductance_kernel(
@@ -30,26 +31,31 @@ def tile_list_airway_series_conductance_kernel(
     nc = tc.nc
     with ExitStack() as ctx:
         keep = ctx.enter_context(tc.tile_pool(name="keep", bufs=1))
+        shared = ctx.enter_context(tc.tile_pool(name="shared", bufs=1))
         psum = ctx.enter_context(tc.psum_pool(name="psum", bufs=1))
 
-        def sb(name, shape, dtype):
-            return keep.tile(shape, dtype, name=name, align_bytes=64)
+        def sb(name, shape, dtype, tag=""):
+            if tag in PLACES:
+                return shared.tile(shape, dtype, name=name, align_bytes=64, offset=PLACES[tag])
+            return keep.tile(shape, dtype, name=name, align_bytes=64, tag=tag)
+
+        def bank(shape, index):
+            return psum.tile(shape, F32, name="bank%d" % index)
 
         offs_t = sb("offs_t", [P, S // 16], U16)
         pos_t = sb("pos_t", [P, M // 16], U16)
         offs2_t = sb("offs2_t", [P, M // 16], U16)
 
         tab_s = sb("tab_s", [P, T], U8)
-        wa_s_raw = sb("wa_s_raw", [P, 2, H], U8)
+        wa_s_raw = sb("wa_s_raw", [P, 2, H], U8, "dealt")
         tab2_s = sb("tab2_s", [P, T2], U8)
-        wf_s = sb("wf_s", [P, N], U8)
+        wf_s = sb("wf_s", [P, 2, N], U8)
         v_s1 = sb("v_s1", [P, S], U8)
         nc.vector.memset(tab_s[:].bitcast(I32), 0)
         nc.gpsimd.memset(wa_s_raw[:].rearrange("p a n -> p (a n)").bitcast(I32), 0)
-        for plane in (tab2_s, wf_s, v_s1):
+        for plane in (v_s1, tab2_s):
             nc.gpsimd.memset(plane[:].bitcast(I32), 0)
-        minus_one = keep.tile([P, 2 * PACK], F32, name="minus_one", tag="column")
-        nc.gpsimd.memset(minus_one[:], -1.0)
+        nc.gpsimd.memset(wf_s[:].rearrange("p a n -> p (a n)").bitcast(I32), 0)
 
         def load_side_by_side(plane, scales):
             for q in range(4):
@@ -58,9 +64,9 @@ def tile_list_airway_series_conductance_kernel(
                     in_=scales[:, 4 * q : 4 * q + 4, :].rearrange("a r n -> r a n").bitcast(I32),
                 )
 
-        def load_packed(plane, scales, queue):
+        def load_packed(plane, scales):
             for q in range(4):
-                queue.dma_start(
+                nc.sync.dma_start(
                     out=plane[32 * q : 32 * q + 8, :].bitcast(I32),
                     in_=scales[:, 4 * q : 4 * q + 4, :].bitcast(I32),
                 )
@@ -70,62 +76,78 @@ def tile_list_airway_series_conductance_kernel(
             nc.sync.dma_start(out=tile[:], in_=words.rearrange("p n i -> p (n i)").bitcast(I32))
             return tile
 
-        def load_wb(a, b):
-            tile = sb("wb_raw%d%d" % (a, b), [P, PACK, KP], F32)
+        def load_both_passes(name, words, tag):
+            tile = sb(name, [P, 2, words.shape[2]], I32, tag)
+            nc.sync.dma_start(out=tile[:], in_=words.rearrange("a p n i -> p a (n i)").bitcast(I32))
+            return tile
+
+        def load_wb(a, b, tag=""):
+            tile = sb("wb_raw%d%d" % (a, b), [P, PACK, KP], F32, tag)
             rows = wb[KP * a : KP * (a + 1), KP * b : KP * (b + 1)]
             nc.sync.dma_start(out=tile[:], in_=rows.rearrange("(p j) c -> p j c", j=PACK))
             return tile
 
-        wa_raw = sb("wa_raw", [P, 2, H // 2], I32)
+        def load_wa(b):
+            tile = sb("wa_raw%d" % b, [P, 2, KP // 2], I32)
+            cols = wa_words[:, :, 2 * KP * b : 2 * KP * (b + 1)]
+            nc.sync.dma_start(out=tile[:], in_=cols.rearrange("a p n -> p a n").bitcast(I32))
+            return tile
+
         nc.sync.dma_start(out=offs_t[:], in_=offs)
-        load_packed(tab_s, tab_scales, nc.sync)
-        nc.sync.dma_start(out=wa_raw[:], in_=wa_words.rearrange("a p n -> p a n").bitcast(I32))
-        wb_raw = {}
+        load_packed(tab_s, tab_scales)
+        wa_raw = [load_wa(0)]
         tab_w = [load_words("tab_w0", tab_words[0])]
-        wb_raw[0, 0] = load_wb(0, 0)
         load_side_by_side(wa_s_raw, wa_scales)
+        wb_raw = {(0, 0): load_wb(0, 0)}
         tab_w.append(load_words("tab_w1", tab_words[1]))
+        wa_raw.append(load_wa(1))
         tab2_w = [load_words("tab2_w%d" % a, tab2_words[a]) for a in range(2)]
         nc.sync.dma_start(out=offs2_t[:], in_=offs2)
-        load_packed(tab2_s, tab2_scales, nc.sync)
+        load_packed(tab2_s, tab2_scales)
         for a, b in ((1, 0), (0, 1), (1, 1)):
             wb_raw[a, b] = load_wb(a, b)
         nc.sync.dma_start(out=pos_t[:], in_=pos1)
         drive_t = sb("drive_t", [P, 2, PACK], F32)
         nc.sync.dma_start(out=drive_t[:], in_=drive.rearrange("(b p t) -> p b t", p=P, t=PACK))
-        load_packed(wf_s, wf_scales, nc.sync)
-        wf_w = sb("wf_w", [P, 2, N], I32)
-        nc.sync.dma_start(
-            out=wf_w[:], in_=wf_words.rearrange("a p n i -> p a (n i)").bitcast(I32)
-        )
-
-        v_s0 = sb("v_s0", [P, S], U8)
-        nc.vector.tensor_copy(out=v_s0[:], in_=tab_s[:].indirect(offs_t[:]))
-        nc.gpsimd.dma_start(out=v_s1[0:112, :].bitcast(I32), in_=v_s0[4:116, :].bitcast(I32))
-        v_s = [v_s0, v_s1]
-
-        wa_w = sb("wa_w", [P, 2, 2 * H], U8)
-        nc.vector.tensor_copy(
-            out=wa_w[:].rearrange("p a n -> p (a n)").bitcast(U16).rearrange(
-                "p (g t c i) -> p g c t i", t=PACK, c=16, i=8),
-            in_=wa_raw[:].rearrange("p a n -> p (a n)").bitcast(U16).rearrange(
-                "p (g c i t) -> p g c t i", t=PACK, c=16, i=8),
-        )
+        load_side_by_side(wf_s, wf_scales)
+        wf_w = load_both_passes("wf_w", wf_words, "")
 
         def gather(name, window, offsets, count, dtype, tag=""):
-            tile = keep.tile([P, count], dtype, name=name, align_bytes=64, tag=tag)
+            tile = sb(name, [P, count], dtype, tag)
             nc.vector.tensor_copy(out=tile[:], in_=window.indirect(offsets))
             return tile
 
-        wb_bf = {}
+        v_s0 = gather("v_s0", tab_s[:], offs_t[:], S, U8)
+        nc.gpsimd.dma_start(out=v_s1[0:112, :].bitcast(I32), in_=v_s0[4:116, :].bitcast(I32))
+        v_s = [v_s0, v_s1]
 
-        def cast_wb(a, b, engine_copy, tag=""):
-            tile = keep.tile([P, KP * PACK], BF16, name="wb_bf%d%d" % (a, b), align_bytes=64, tag=tag)
-            engine_copy(
-                out=tile[:].rearrange("p (t m j) -> p m t j", t=PACK, j=PACK),
-                in_=wb_raw[a, b][:].rearrange("p j (m t) -> p m t j", t=PACK),
+        def deal_wa(b):
+            tile = sb("wa_w%d" % b, [P, 2, 2 * KP], U8)
+            nc.vector.tensor_copy(
+                out=tile[:].rearrange("p a n -> p (a n)").bitcast(U16).rearrange(
+                    "p (a t c i) -> p a c t i", t=PACK, c=16, i=8),
+                in_=wa_raw[b][:].rearrange("p a n -> p (a n)").bitcast(U16).rearrange(
+                    "p (a c i t) -> p a c t i", t=PACK, c=16, i=8),
             )
-            wb_bf[a, b] = tile
+            return tile
+
+        v_w = {}
+
+        def gather_tab(a, h, tag=""):
+            v_w[a, h] = gather("v_w%d%d" % (a, h), tab_w[a][:].bitcast(U32),
+                               offs_t[:, 32 * h : 32 * (h + 1)], BANK, U32, tag)
+
+        wa_w = [deal_wa(0)]
+        gather_tab(0, 0)
+        wa_s = sb("wa_s", [P, 2, H], U8)
+        nc.vector.tensor_copy(
+            out=wa_s[:].rearrange("p a (b t c i) -> p (a b) c t i", t=PACK, c=8, i=16),
+            in_=wa_s_raw[:].rearrange("p a (b c i t) -> p (a b) c t i", t=PACK, c=8, i=16),
+        )
+        gather_tab(0, 1, "dealt")
+        for h in range(2):
+            gather_tab(1, h)
+        wa_w.append(deal_wa(1))
 
         def quantize(name, src, words):
             codes = sb(name + "_w", [P, words], U32)
@@ -133,37 +155,32 @@ def tile_list_airway_series_conductance_kernel(
             nc.vector.quantize_mx(out=codes[:].bitcast(FP8X4), scales=scales[:], in_=src)
             return codes, scales
 
-        cast_wb(0, 0, nc.scalar.copy)
-        v_w = {}
+        def cast_wb(a, b, engine_copy):
+            tile = sb("wb_bf%d%d" % (a, b), [P, KP * PACK], BF16)
+            engine_copy(
+                out=tile[:].rearrange("p (t m j) -> p m t j", t=PACK, j=PACK),
+                in_=wb_raw[a, b][:].rearrange("p j (m t) -> p m t j", t=PACK),
+            )
+            return tile
 
-        def gather_pass(a):
-            for h in range(2):
-                v_w[a, h] = gather("v_w%d%d" % (a, h), tab_w[a][:].bitcast(U32),
-                                   offs_t[:, 32 * h : 32 * (h + 1)], BANK, U32)
-
-        gather_pass(0)
-        wa_s = keep.tile([P, 2, H], U8, name="wa_s", align_bytes=64, tag="tab_w0")
-        nc.vector.tensor_copy(
-            out=wa_s[:].rearrange("p a (b t c i) -> p (a b) c t i", t=PACK, c=8, i=16),
-            in_=wa_s_raw[:].rearrange("p a (b c i t) -> p (a b) c t i", t=PACK, c=8, i=16),
-        )
-        gather_pass(1)
+        first = cast_wb(0, 0, nc.scalar.copy)
         v2_w = [gather("v2_w%d" % a, tab2_w[a][:].bitcast(U32), offs2_t[:], M, U32) for a in range(2)]
         v2_s = gather("v2_s", tab2_s[:], offs2_t[:], M, U8)
-        wb_q = {}
+        wb_q = {(0, 0): quantize("wb_q00", first[:], KP)}
+        for a, b in ((1, 0), (0, 1), (1, 1)):
+            wb_q[a, b] = quantize("wb_q%d%d" % (a, b), cast_wb(a, b, nc.vector.tensor_copy)[:], KP)
 
-        ra, rb = {}, {}
+        ra = {(b, t): sb("ra%d%d" % (b, t), [P, S], F32) for b in range(2) for t in range(PACK)}
+        rb = {(b, t): sb("rb%d%d" % (b, t), [P, M], F32) for b in range(2) for t in range(PACK)}
 
-        def make_ra(b, t, h):
-            if h == 0:
-                ra[b, t] = sb("ra%d%d" % (b, t), [P, S], F32)
+        def make_ra(b, t, h, index):
             c0 = KP * b + P * t
             cols = slice(BANK * h, BANK * (h + 1))
-            acc = psum.tile([P, BANK], F32, name="acc", bufs=8)
+            acc = bank([P, BANK], index)
             for a in range(2):
                 nc.tensor.matmul_mx(
                     out=acc[:],
-                    lhsT=wa_w[:, a, 2 * c0 : 2 * (c0 + P)].bitcast(FP4X4),
+                    lhsT=wa_w[b][:, a, 2 * P * t : 2 * P * (t + 1)].bitcast(FP4X4),
                     lhsT_scale=wa_s[:, a, c0 : c0 + P],
                     rhs=v_w[a, h][:].bitcast(FP8X4),
                     rhs_scale=v_s[a][:, cols],
@@ -172,9 +189,8 @@ def tile_list_airway_series_conductance_kernel(
             nc.scalar.activation(out=ra[b, t][:, cols], in_=acc[:], func=ACT.Exp, scale=-1.0)
 
         def make_rb(b, t):
-            tile = sb("rb%d%d" % (b, t), [P, M], F32)
+            acc = bank([P, BANK], (PACK * b + t + 4) % 8)
             cols = slice(P * t, P * (t + 1))
-            acc = psum.tile([P, BANK], F32, name="acc", bufs=8)
             for a in range(2):
                 codes, scales = wb_q[a, b]
                 nc.tensor.matmul_mx(
@@ -185,12 +201,21 @@ def tile_list_airway_series_conductance_kernel(
                     rhs_scale=v2_s[4 * a : P, :],
                     start=(a == 0), stop=(a == 1),
                 )
-            scale = minus_one[:, 0:1] if b == 1 else -1.0
-            nc.scalar.activation(out=tile[:], in_=acc[:], func=ACT.Exp, scale=scale)
-            rb[b, t] = tile
+            nc.scalar.activation(out=rb[b, t][:], in_=acc[:], func=ACT.Exp, scale=-1.0)
 
-        def make_series(b, c0, width, tag):
-            tile = keep.tile([P, PACK, width], F32, name="series%d_%d" % (b, c0), align_bytes=64, tag=tag)
+        for b in range(2):
+            for h in range(2):
+                for t in range(PACK):
+                    make_ra(b, t, h, (8 * b + PACK * h + t) % 6)
+        for b in range(2):
+            for t in range(PACK):
+                make_rb(b, t)
+
+        inv_drive = sb("inv_drive", [P, 2 * PACK], F32, "wb_q11_s")
+        nc.vector.reciprocal(out=inv_drive[:], in_=drive_t[:].rearrange("p b t -> p (b t)"))
+
+        def make_series(b, c0, width, tag=""):
+            tile = sb("series%d_%d" % (b, c0), [P, PACK, width], F32, tag)
             for t in range(PACK):
                 nc.vector.tensor_tensor(
                     out=tile[:, t, :],
@@ -200,8 +225,8 @@ def tile_list_airway_series_conductance_kernel(
                 )
             return tile
 
-        def make_root(b, h, series):
-            root = sb("root%d%d" % (b, h), [P, PACK, HALF], F32)
+        def make_root(b, c0, series, tag=""):
+            root = sb("root%d_%d" % (b, c0), series.shape, F32, tag)
             for t in range(PACK):
                 s = PACK * b + t
                 nc.scalar.activation(
@@ -210,67 +235,55 @@ def tile_list_airway_series_conductance_kernel(
                 )
             return root
 
-        def make_z(b, h, root, on_vector):
-            z_bf = sb("z_bf%d%d" % (b, h), [P, HALF * PACK], BF16)
+        def make_z(b, c0, root, on_vector):
+            width = root.shape[2]
+            z_bf = sb("z_bf%d_%d" % (b, c0), [P, width * PACK], BF16)
             dst = z_bf[:].rearrange("p (c i t) -> p c t i", i=4, t=PACK)
             src = root[:].rearrange("p t (c i) -> p c t i", i=4)
             if on_vector:
                 nc.vector.tensor_tensor(out=dst, in0=src, in1=src, op=ALU.mult)
             else:
                 nc.scalar.activation(out=dst, in_=src, func=ACT.Square)
-            return quantize("z_q%d%d" % (b, h), z_bf[:], HALF)
+            return quantize("z_q%d_%d" % (b, c0), z_bf[:], width)
 
-        for h in range(2):
-            for t in range(PACK):
-                make_ra(0, t, h)
-        cast_wb(1, 0, nc.vector.tensor_copy, tag="tab2_w0")
-        for a in range(2):
-            wb_q[a, 0] = quantize("wb_q%d0" % a, wb_bf[a, 0][:], KP)
-        cast_wb(0, 1, nc.vector.tensor_copy, tag="tab2_w1")
-        cast_wb(1, 1, nc.vector.tensor_copy, tag="tab2_w0")
-        for a in range(2):
-            wb_q[a, 1] = quantize("wb_q%d1" % a, wb_bf[a, 1][:], KP)
-        inv_early = sb("inv_early", [P, 2 * PACK], F32)
-        nc.vector.reciprocal(out=inv_early[:], in_=drive_t[:].rearrange("p b t -> p (b t)"))
-        for t in range(2):
-            for h in range(2):
-                make_ra(1, t, h)
-        for t in range(PACK):
-            make_rb(0, t)
-        for t in range(2, PACK):
-            for h in range(2):
-                make_ra(1, t, h)
-        series0 = make_series(0, 0, M, "tab2_w0")
-        for t in range(PACK):
-            make_rb(1, t)
-        inv_drive = keep.tile([P, 2 * PACK], F32, name="inv_drive", tag="column")
-        nc.scalar.copy(out=inv_drive[:], in_=inv_early[:])
-        series = {(0, h): series0[:, :, HALF * h : HALF * (h + 1)] for h in range(2)}
-        series[1, 0] = make_series(1, 0, HALF, "series1")
-        series[1, 1] = make_series(1, HALF, HALF, "wb_q11_w")
-        results = []
+        groups = {0: ((0, 1), (2, 3)), 256: ((0, 1, 2, 3),), 384: ((0, 1), (2, 3))}
+        accs = {}
 
-        for h in range(2):
-            mcols = slice(HALF * h, HALF * (h + 1))
-            accs = [psum.tile([P, BANK], F32, name="acc", bufs=8) for j in range(4)]
-            for b in range(2):
-                codes, scales = make_z(b, h, make_root(b, h, series[b, h]), on_vector=(b != h))
-                for j in range(4):
+        def multiply(b, c0, width, z_q, z0):
+            codes, scales = z_q
+            for js in groups[c0]:
+                if b == 0:
+                    accs[c0, js] = bank([P, len(js), width], len(accs))
+                for i, j in enumerate(js):
                     ncols = slice(P * j, P * (j + 1))
                     nc.tensor.matmul_mx(
-                        out=accs[j][:, 0:HALF],
+                        out=accs[c0, js][:, i, :],
                         lhsT=wf_w[:, b, ncols].bitcast(FP8X4),
-                        lhsT_scale=wf_s[4 * b : P, ncols],
-                        rhs=codes[:].bitcast(FP8X4),
-                        rhs_scale=scales[:],
-                        start=(b == 0), stop=(b == 1),
+                        lhsT_scale=wf_s[:, b, ncols],
+                        rhs=codes[:, c0 - z0 : c0 - z0 + width].bitcast(FP8X4),
+                        rhs_scale=scales[:, c0 - z0 : c0 - z0 + width],
+                        start=(b == 0 and i == 0), stop=(b == 1 and i == len(js) - 1),
                     )
-            results.append((accs, mcols))
-        for h, (accs, mcols) in enumerate(results):
-            for pair in range(2):
-                res = sb("res%d%d" % (h, pair), [P, 2, HALF], F32)
-                copies = (nc.scalar.copy if h == 0 else nc.vector.tensor_copy, nc.scalar.copy)
-                for i, engine_copy in enumerate(copies):
-                    engine_copy(out=res[:, i, :], in_=accs[2 * pair + i][:, 0:HALF])
-                rows = out[2 * P * pair : 2 * P * (pair + 1), mcols]
+
+        series = {(0, 0): make_series(0, 0, 256, "wb_raw11")}
+        series[1, 0] = make_series(1, 0, 256)
+        series[0, 256] = make_series(0, 256, 256)
+        for b in range(2):
+            root = make_root(b, 0, series[b, 0])
+            multiply(b, 0, 256, make_z(b, 0, root, on_vector=False), 0)
+        series[1, 256] = make_series(1, 256, 128, "z_bf0_0")
+        series[1, 384] = make_series(1, 384, 128)
+        roots = {key: make_root(key[0], key[1], series[key]) for key in ((0, 256), (1, 256), (1, 384))}
+        z_q = make_z(0, 256, roots[0, 256], on_vector=True)
+        for c0, width in CHUNKS[1:]:
+            multiply(0, c0, width, z_q, 256)
+        for c0, width in CHUNKS[1:]:
+            multiply(1, c0, width, make_z(1, c0, roots[1, c0], on_vector=(c0 == 256)), c0)
+        copies = {0: (nc.scalar.copy, nc.scalar.copy), 256: (nc.vector.tensor_copy,),
+                  384: (nc.vector.tensor_copy, nc.scalar.copy)}
+        for c0, width in CHUNKS:
+            for js, engine_copy in zip(groups[c0], copies[c0]):
+                res = sb("res%d_%d" % (c0, js[0]), [P, len(js), width], F32)
+                engine_copy(out=res[:], in_=accs[c0, js][:])
+                rows = out[P * js[0] : P * (js[-1] + 1), c0 : c0 + width]
                 nc.sync.dma_start(out=rows.rearrange("(j p) m -> p j m", p=P), in_=res[:])

@@ -57,9 +57,9 @@ def tile_list_airway_series_conductance_kernel(
             nc.gpsimd.memset(plane[:].bitcast(I32), 0)
         nc.gpsimd.memset(wf_s[:].rearrange("p a n -> p (a n)").bitcast(I32), 0)
 
-        def load_side_by_side(plane, scales):
+        def load_side_by_side(plane, scales, queue):
             for q in range(4):
-                nc.sync.dma_start(
+                queue.dma_start(
                     out=plane[32 * q : 32 * q + 4, :, :].bitcast(I32),
                     in_=scales[:, 4 * q : 4 * q + 4, :].rearrange("a r n -> r a n").bitcast(I32),
                 )
@@ -93,13 +93,27 @@ def tile_list_airway_series_conductance_kernel(
             nc.sync.dma_start(out=tile[:], in_=cols.rearrange("a p n -> p a n").bitcast(I32))
             return tile
 
-        nc.sync.dma_start(out=offs_t[:], in_=offs)
-        load_packed(tab_s, tab_scales)
         wa_raw = [load_wa(0)]
+        nc.sync.dma_start(out=offs_t[:], in_=offs)
+        for q in range(4):
+            nc.sync.dma_start(out=tab_s[32 * q : 32 * q + 4, :].bitcast(I32),
+                                in_=tab_scales[0, 4 * q : 4 * q + 4, :].bitcast(I32))
+        nc.sync.dma_start(out=tab_s[4:P:8, :].bitcast(I32), in_=tab_scales[1].bitcast(I32))
         tab_w = [load_words("tab_w0", tab_words[0])]
-        load_side_by_side(wa_s_raw, wa_scales)
+        load_side_by_side(wa_s_raw, wa_scales, nc.sync)
         wb_raw = {(0, 0): load_wb(0, 0)}
         tab_w.append(load_words("tab_w1", tab_words[1]))
+
+        def gather(name, window, offsets, count, dtype, tag=""):
+            tile = sb(name, [P, count], dtype, tag)
+            nc.vector.tensor_copy(out=tile[:], in_=window.indirect(offsets))
+            return tile
+
+        v_s0 = gather("v_s0", tab_s[:], offs_t[:], S, U8)
+        for r in range(4):
+            nc.sync.dma_start(out=v_s1[r:P:32, :].bitcast(I32), in_=v_s0[4 + 8 * r : P : 32, :].bitcast(I32))
+        v_s = [v_s0, v_s1]
+
         wa_raw.append(load_wa(1))
         tab2_w = [load_words("tab2_w%d" % a, tab2_words[a]) for a in range(2)]
         nc.sync.dma_start(out=offs2_t[:], in_=offs2)
@@ -109,17 +123,8 @@ def tile_list_airway_series_conductance_kernel(
         nc.sync.dma_start(out=pos_t[:], in_=pos1)
         drive_t = sb("drive_t", [P, 2, PACK], F32)
         nc.sync.dma_start(out=drive_t[:], in_=drive.rearrange("(b p t) -> p b t", p=P, t=PACK))
-        load_side_by_side(wf_s, wf_scales)
+        load_side_by_side(wf_s, wf_scales, nc.sync)
         wf_w = load_both_passes("wf_w", wf_words, "")
-
-        def gather(name, window, offsets, count, dtype, tag=""):
-            tile = sb(name, [P, count], dtype, tag)
-            nc.vector.tensor_copy(out=tile[:], in_=window.indirect(offsets))
-            return tile
-
-        v_s0 = gather("v_s0", tab_s[:], offs_t[:], S, U8)
-        nc.gpsimd.dma_start(out=v_s1[0:112, :].bitcast(I32), in_=v_s0[4:116, :].bitcast(I32))
-        v_s = [v_s0, v_s1]
 
         def deal_wa(b):
             tile = sb("wa_w%d" % b, [P, 2, 2 * KP], U8)

@@ -21,7 +21,7 @@ PACK = 4
 KP = P * PACK
 BANK = 512
 PLACES = {"dealt": 0}
-CHUNKS = ((0, 256), (256, 128), (384, 128))
+HALF = M // 2
 
 
 def tile_list_airway_series_conductance_kernel(
@@ -163,8 +163,8 @@ def tile_list_airway_series_conductance_kernel(
         def cast_wb(a, b, engine_copy):
             tile = sb("wb_bf%d%d" % (a, b), [P, KP * PACK], BF16)
             engine_copy(
-                out=tile[:].rearrange("p (t m j) -> p m t j", t=PACK, j=PACK),
-                in_=wb_raw[a, b][:].rearrange("p j (m t) -> p m t j", t=PACK),
+                out=tile[:].rearrange("p (t m j) -> p m j t", t=PACK, j=PACK),
+                in_=wb_raw[a, b][:].rearrange("p j (m t) -> p m j t", t=PACK),
             )
             return tile
 
@@ -231,7 +231,7 @@ def tile_list_airway_series_conductance_kernel(
             return tile
 
         def make_root(b, c0, series, tag=""):
-            root = sb("root%d_%d" % (b, c0), series.shape, F32, tag)
+            root = sb("root%d_%d" % (b, c0), [P, PACK, HALF], F32, tag)
             for t in range(PACK):
                 s = PACK * b + t
                 nc.scalar.activation(
@@ -251,44 +251,31 @@ def tile_list_airway_series_conductance_kernel(
                 nc.scalar.activation(out=dst, in_=src, func=ACT.Square)
             return quantize("z_q%d_%d" % (b, c0), z_bf[:], width)
 
-        groups = {0: ((0, 1), (2, 3)), 256: ((0, 1, 2, 3),), 384: ((0, 1), (2, 3))}
-        accs = {}
-
-        def multiply(b, c0, width, z_q, z0):
-            codes, scales = z_q
-            for js in groups[c0]:
-                if b == 0:
-                    accs[c0, js] = bank([P, len(js), width], len(accs))
-                for i, j in enumerate(js):
+        series0 = make_series(0, 0, M, "wb_raw11")
+        series = {(0, h): series0[:, :, HALF * h : HALF * (h + 1)] for h in range(2)}
+        for h in range(2):
+            series[1, h] = make_series(1, HALF * h, HALF)[:]
+        results = []
+        for h in range(2):
+            accs = [bank([P, HALF], PACK * h + j) for j in range(4)]
+            for b in range(2):
+                codes, scales = make_z(b, h, make_root(b, h, series[b, h]), on_vector=(b != h))
+                for j in range(4):
                     ncols = slice(P * j, P * (j + 1))
                     nc.tensor.matmul_mx(
-                        out=accs[c0, js][:, i, :],
+                        out=accs[j][:],
                         lhsT=wf_w[:, b, ncols].bitcast(FP8X4),
                         lhsT_scale=wf_s[:, b, ncols],
-                        rhs=codes[:, c0 - z0 : c0 - z0 + width].bitcast(FP8X4),
-                        rhs_scale=scales[:, c0 - z0 : c0 - z0 + width],
-                        start=(b == 0 and i == 0), stop=(b == 1 and i == len(js) - 1),
+                        rhs=codes[:].bitcast(FP8X4),
+                        rhs_scale=scales[:],
+                        start=(b == 0), stop=(b == 1),
                     )
-
-        series = {(0, 0): make_series(0, 0, 256, "wb_raw11")}
-        series[1, 0] = make_series(1, 0, 256)
-        series[0, 256] = make_series(0, 256, 256)
-        for b in range(2):
-            root = make_root(b, 0, series[b, 0])
-            multiply(b, 0, 256, make_z(b, 0, root, on_vector=False), 0)
-        series[1, 256] = make_series(1, 256, 128, "z_bf0_0")
-        series[1, 384] = make_series(1, 384, 128)
-        roots = {key: make_root(key[0], key[1], series[key]) for key in ((0, 256), (1, 256), (1, 384))}
-        z_q = make_z(0, 256, roots[0, 256], on_vector=True)
-        for c0, width in CHUNKS[1:]:
-            multiply(0, c0, width, z_q, 256)
-        for c0, width in CHUNKS[1:]:
-            multiply(1, c0, width, make_z(1, c0, roots[1, c0], on_vector=(c0 == 256)), c0)
-        copies = {0: (nc.scalar.copy, nc.scalar.copy), 256: (nc.vector.tensor_copy,),
-                  384: (nc.vector.tensor_copy, nc.scalar.copy)}
-        for c0, width in CHUNKS:
-            for js, engine_copy in zip(groups[c0], copies[c0]):
-                res = sb("res%d_%d" % (c0, js[0]), [P, len(js), width], F32)
-                engine_copy(out=res[:], in_=accs[c0, js][:])
-                rows = out[P * js[0] : P * (js[-1] + 1), c0 : c0 + width]
+            results.append(accs)
+        for h, accs in enumerate(results):
+            for pair in range(2):
+                res = sb("res%d%d" % (h, pair), [P, 2, HALF], F32)
+                copies = (nc.scalar.copy if h == 0 else nc.vector.tensor_copy, nc.scalar.copy)
+                for i, engine_copy in enumerate(copies):
+                    engine_copy(out=res[:, i, :], in_=accs[2 * pair + i][:])
+                rows = out[2 * P * pair : 2 * P * (pair + 1), HALF * h : HALF * (h + 1)]
                 nc.sync.dma_start(out=rows.rearrange("(j p) m -> p j m", p=P), in_=res[:])

@@ -20,7 +20,6 @@ P = 128
 PACK = 4
 KP = P * PACK
 BANK = 512
-PLACES = {"dealt": 0}
 HALF = M // 2
 
 
@@ -31,12 +30,9 @@ def tile_list_airway_series_conductance_kernel(
     nc = tc.nc
     with ExitStack() as ctx:
         keep = ctx.enter_context(tc.tile_pool(name="keep", bufs=1))
-        shared = ctx.enter_context(tc.tile_pool(name="shared", bufs=1))
         psum = ctx.enter_context(tc.psum_pool(name="psum", bufs=1))
 
         def sb(name, shape, dtype, tag=""):
-            if tag in PLACES:
-                return shared.tile(shape, dtype, name=name, align_bytes=64, offset=PLACES[tag])
             return keep.tile(shape, dtype, name=name, align_bytes=64, tag=tag)
 
         def bank(shape, index):
@@ -47,29 +43,34 @@ def tile_list_airway_series_conductance_kernel(
         offs2_t = sb("offs2_t", [P, M // 16], U16)
 
         tab_s = sb("tab_s", [P, T], U8)
-        wa_s_raw = sb("wa_s_raw", [P, 2, H], U8, "dealt")
+        wa_s_raw = sb("wa_s_raw", [P, 2, H], U8)
         tab2_s = sb("tab2_s", [P, T2], U8)
+        v2_s = sb("v2_s", [P, 2, M], U8)
         wf_s = sb("wf_s", [P, 2, N], U8)
-        v_s1 = sb("v_s1", [P, S], U8)
-        nc.vector.memset(tab_s[:].bitcast(I32), 0)
+        v_s = sb("v_s", [P, 2, S], U8)
+        nc.vector.memset(tab_s[0:96, :].bitcast(I32), 0)
         nc.gpsimd.memset(wa_s_raw[:].rearrange("p a n -> p (a n)").bitcast(I32), 0)
-        for plane in (v_s1, tab2_s):
-            nc.gpsimd.memset(plane[:].bitcast(I32), 0)
+        nc.gpsimd.memset(v_s[:].rearrange("p a n -> p (a n)").bitcast(I32), 0)
+        nc.gpsimd.memset(tab2_s[0:96, :].bitcast(I32), 0)
+        nc.gpsimd.memset(v2_s[:].rearrange("p a n -> p (a n)").bitcast(I32), 0)
         nc.gpsimd.memset(wf_s[:].rearrange("p a n -> p (a n)").bitcast(I32), 0)
 
-        def load_side_by_side(plane, scales, queue):
+        def load_side_by_side(plane, scales, first):
             for q in range(4):
-                queue.dma_start(
-                    out=plane[32 * q : 32 * q + 4, :, :].bitcast(I32),
+                nc.sync.dma_start(
+                    out=plane[32 * q + first : 32 * q + first + 4, :, :].bitcast(I32),
                     in_=scales[:, 4 * q : 4 * q + 4, :].rearrange("a r n -> r a n").bitcast(I32),
                 )
 
-        def load_packed(plane, scales):
+        def load_rows(window, scales):
+            nc.sync.dma_start(out=window[96:P, :].bitcast(I32),
+                              in_=scales.rearrange("a q n -> q a n").bitcast(I32))
+
+        def move_rows(plane, rows, first):
             for q in range(4):
                 nc.sync.dma_start(
-                    out=plane[32 * q : 32 * q + 8, :].bitcast(I32),
-                    in_=scales[:, 4 * q : 4 * q + 4, :].bitcast(I32),
-                )
+                    out=plane[32 * q + first : 32 * q + first + 4, :, :].rearrange("p a n -> p (a n)").bitcast(I32),
+                    in_=rows[96 + 8 * q : 104 + 8 * q, :].bitcast(I32))
 
         def load_words(name, words):
             tile = sb(name, [P, words.shape[1]], I32)
@@ -93,16 +94,15 @@ def tile_list_airway_series_conductance_kernel(
             nc.sync.dma_start(out=tile[:], in_=cols.rearrange("a p n -> p a n").bitcast(I32))
             return tile
 
-        wa_raw = [load_wa(0)]
+        load_rows(tab_s, tab_scales)
         nc.sync.dma_start(out=offs_t[:], in_=offs)
-        for q in range(4):
-            nc.sync.dma_start(out=tab_s[32 * q : 32 * q + 4, :].bitcast(I32),
-                                in_=tab_scales[0, 4 * q : 4 * q + 4, :].bitcast(I32))
-        nc.sync.dma_start(out=tab_s[4:P:8, :].bitcast(I32), in_=tab_scales[1].bitcast(I32))
+        wa_raw = [load_wa(0)]
+        load_side_by_side(wa_s_raw, wa_scales, 0)
         tab_w = [load_words("tab_w0", tab_words[0])]
-        load_side_by_side(wa_s_raw, wa_scales, nc.sync)
+        wa_raw.append(load_wa(1))
+        load_rows(tab2_s, tab2_scales)
+        nc.sync.dma_start(out=offs2_t[:], in_=offs2)
         wb_raw = {(0, 0): load_wb(0, 0)}
-        tab_w.append(load_words("tab_w1", tab_words[1]))
 
         def gather(name, window, offsets, count, dtype, tag=""):
             tile = sb(name, [P, count], dtype, tag)
@@ -110,21 +110,10 @@ def tile_list_airway_series_conductance_kernel(
             return tile
 
         v_s0 = gather("v_s0", tab_s[:], offs_t[:], S, U8)
-        for r in range(4):
-            nc.sync.dma_start(out=v_s1[r:P:32, :].bitcast(I32), in_=v_s0[4 + 8 * r : P : 32, :].bitcast(I32))
-        v_s = [v_s0, v_s1]
-
-        wa_raw.append(load_wa(1))
+        move_rows(v_s, v_s0, 0)
+        tab_w.append(load_words("tab_w1", tab_words[1]))
         tab2_w = [load_words("tab2_w%d" % a, tab2_words[a]) for a in range(2)]
-        nc.sync.dma_start(out=offs2_t[:], in_=offs2)
-        load_packed(tab2_s, tab2_scales)
-        for a, b in ((1, 0), (0, 1), (1, 1)):
-            wb_raw[a, b] = load_wb(a, b)
-        nc.sync.dma_start(out=pos_t[:], in_=pos1)
-        drive_t = sb("drive_t", [P, 2, PACK], F32)
-        nc.sync.dma_start(out=drive_t[:], in_=drive.rearrange("(b p t) -> p b t", p=P, t=PACK))
-        load_side_by_side(wf_s, wf_scales, nc.sync)
-        wf_w = load_both_passes("wf_w", wf_words, "")
+        wb_raw[1, 0] = load_wb(1, 0)
 
         def deal_wa(b):
             tile = sb("wa_w%d" % b, [P, 2, 2 * KP], U8)
@@ -149,10 +138,19 @@ def tile_list_airway_series_conductance_kernel(
             out=wa_s[:].rearrange("p a (b t c i) -> p (a b) c t i", t=PACK, c=8, i=16),
             in_=wa_s_raw[:].rearrange("p a (b c i t) -> p (a b) c t i", t=PACK, c=8, i=16),
         )
-        gather_tab(0, 1, "dealt")
+        gather_tab(0, 1)
+        wa_w.append(deal_wa(1))
+        v2_s0 = gather("v2_s0", tab2_s[:], offs2_t[:], M, U8)
+        move_rows(v2_s, v2_s0, 4)
+        wb_raw[0, 1] = load_wb(0, 1)
+        nc.sync.dma_start(out=pos_t[:], in_=pos1)
+        drive_t = sb("drive_t", [P, 2, PACK], F32)
+        nc.sync.dma_start(out=drive_t[:], in_=drive.rearrange("(b p t) -> p b t", p=P, t=PACK))
+        wb_raw[1, 1] = load_wb(1, 1)
+        wf_w = load_both_passes("wf_w", wf_words, "")
+        load_side_by_side(wf_s, wf_scales, 8)
         for h in range(2):
             gather_tab(1, h)
-        wa_w.append(deal_wa(1))
 
         def quantize(name, src, words):
             codes = sb(name + "_w", [P, words], U32)
@@ -170,7 +168,6 @@ def tile_list_airway_series_conductance_kernel(
 
         first = cast_wb(0, 0, nc.scalar.copy)
         v2_w = [gather("v2_w%d" % a, tab2_w[a][:].bitcast(U32), offs2_t[:], M, U32) for a in range(2)]
-        v2_s = gather("v2_s", tab2_s[:], offs2_t[:], M, U8)
         wb_q = {(0, 0): quantize("wb_q00", first[:], KP)}
         for a, b in ((1, 0), (0, 1), (1, 1)):
             wb_q[a, b] = quantize("wb_q%d%d" % (a, b), cast_wb(a, b, nc.vector.tensor_copy)[:], KP)
@@ -188,7 +185,7 @@ def tile_list_airway_series_conductance_kernel(
                     lhsT=wa_w[b][:, a, 2 * P * t : 2 * P * (t + 1)].bitcast(FP4X4),
                     lhsT_scale=wa_s[:, a, c0 : c0 + P],
                     rhs=v_w[a, h][:].bitcast(FP8X4),
-                    rhs_scale=v_s[a][:, cols],
+                    rhs_scale=v_s[:, a, cols],
                     start=(a == 0), stop=(a == 1),
                 )
             nc.scalar.activation(out=ra[b, t][:, cols], in_=acc[:], func=ACT.Exp, scale=-1.0)
@@ -203,7 +200,7 @@ def tile_list_airway_series_conductance_kernel(
                     lhsT=codes[:, cols].bitcast(FP8X4),
                     lhsT_scale=scales[:, cols],
                     rhs=v2_w[a][:].bitcast(FP8X4),
-                    rhs_scale=v2_s[4 * a : P, :],
+                    rhs_scale=v2_s[4:P, a, :],
                     start=(a == 0), stop=(a == 1),
                 )
             nc.scalar.activation(out=rb[b, t][:], in_=acc[:], func=ACT.Exp, scale=-1.0)
@@ -265,7 +262,7 @@ def tile_list_airway_series_conductance_kernel(
                     nc.tensor.matmul_mx(
                         out=accs[j][:],
                         lhsT=wf_w[:, b, ncols].bitcast(FP8X4),
-                        lhsT_scale=wf_s[:, b, ncols],
+                        lhsT_scale=wf_s[8:P, b, ncols],
                         rhs=codes[:].bitcast(FP8X4),
                         rhs_scale=scales[:],
                         start=(b == 0), stop=(b == 1),

@@ -88,8 +88,8 @@ def tile_list_airway_series_conductance_kernel(
             nc.sync.dma_start(out=tile[:], in_=rows.rearrange("(p j) c -> p j c", j=PACK))
             return tile
 
-        def load_wa(b):
-            tile = sb("wa_raw%d" % b, [P, 2, KP // 2], I32)
+        def load_wa(b, tag=""):
+            tile = sb("wa_raw%d" % b, [P, 2, KP // 2], I32, tag)
             cols = wa_words[:, :, 2 * KP * b : 2 * KP * (b + 1)]
             nc.sync.dma_start(out=tile[:], in_=cols.rearrange("a p n -> p a n").bitcast(I32))
             return tile
@@ -99,10 +99,7 @@ def tile_list_airway_series_conductance_kernel(
         wa_raw = [load_wa(0)]
         load_side_by_side(wa_s_raw, wa_scales, 0)
         tab_w = [load_words("tab_w0", tab_words[0])]
-        wa_raw.append(load_wa(1))
-        load_rows(tab2_s, tab2_scales)
-        nc.sync.dma_start(out=offs2_t[:], in_=offs2)
-        wb_raw = {(0, 0): load_wb(0, 0)}
+        tab_w.append(load_words("tab_w1", tab_words[1]))
 
         def gather(name, window, offsets, count, dtype, tag=""):
             tile = sb(name, [P, count], dtype, tag)
@@ -111,7 +108,10 @@ def tile_list_airway_series_conductance_kernel(
 
         v_s0 = gather("v_s0", tab_s[:], offs_t[:], S, U8)
         move_rows(v_s, v_s0, 0)
-        tab_w.append(load_words("tab_w1", tab_words[1]))
+        wa_raw.append(load_wa(1, "late"))
+        wb_raw = {(0, 0): load_wb(0, 0)}
+        load_rows(tab2_s, tab2_scales)
+        nc.sync.dma_start(out=offs2_t[:], in_=offs2)
         tab2_w = [load_words("tab2_w%d" % a, tab2_words[a]) for a in range(2)]
         wb_raw[1, 0] = load_wb(1, 0)
 
@@ -139,7 +139,9 @@ def tile_list_airway_series_conductance_kernel(
             in_=wa_s_raw[:].rearrange("p a (b c i t) -> p (a b) c t i", t=PACK, c=8, i=16),
         )
         gather_tab(0, 1)
+        gather_tab(1, 0)
         wa_w.append(deal_wa(1))
+        gather_tab(1, 1)
         v2_s0 = gather("v2_s0", tab2_s[:], offs2_t[:], M, U8)
         move_rows(v2_s, v2_s0, 4)
         wb_raw[0, 1] = load_wb(0, 1)
@@ -149,26 +151,30 @@ def tile_list_airway_series_conductance_kernel(
         wb_raw[1, 1] = load_wb(1, 1)
         wf_w = load_both_passes("wf_w", wf_words, "")
         load_side_by_side(wf_s, wf_scales, 8)
-        for h in range(2):
-            gather_tab(1, h)
 
-        def quantize(name, src, words):
-            codes = sb(name + "_w", [P, words], U32)
+        def quantize(name, src, words, tag=""):
+            codes = sb(name + "_w", [P, words], U32, tag)
             scales = sb(name + "_s", [P, words], U8)
             nc.vector.quantize_mx(out=codes[:].bitcast(FP8X4), scales=scales[:], in_=src)
             return codes, scales
 
-        def cast_wb(a, b, engine_copy):
-            tile = sb("wb_bf%d%d" % (a, b), [P, KP * PACK], BF16)
+        def cast_wb(a, b, engine_copy, tag=""):
+            tile = sb("wb_bf%d%d" % (a, b), [P, KP * PACK], BF16, tag)
             engine_copy(
                 out=tile[:].rearrange("p (t m j) -> p m j t", t=PACK, j=PACK),
                 in_=wb_raw[a, b][:].rearrange("p j (m t) -> p m j t", t=PACK),
             )
             return tile
 
-        first = cast_wb(0, 0, nc.scalar.copy)
+        def pool_copy(out, in_):
+            for half in range(2):
+                rows = slice(64 * half, 64 * (half + 1))
+                nc.gpsimd.tensor_copy(out=out[:, rows].rearrange("p m j t -> p m t j"),
+                                      in_=in_[:, rows].rearrange("p m j t -> p m t j"))
+
+        first = cast_wb(0, 0, pool_copy, "late")
         v2_w = [gather("v2_w%d" % a, tab2_w[a][:].bitcast(U32), offs2_t[:], M, U32) for a in range(2)]
-        wb_q = {(0, 0): quantize("wb_q00", first[:], KP)}
+        wb_q = {(0, 0): quantize("wb_q00", first[:], KP, "tab2_w1")}
         for a, b in ((1, 0), (0, 1), (1, 1)):
             wb_q[a, b] = quantize("wb_q%d%d" % (a, b), cast_wb(a, b, nc.vector.tensor_copy)[:], KP)
 

@@ -88,15 +88,22 @@ def tile_list_airway_series_conductance_kernel(
             nc.sync.dma_start(out=tile[:], in_=rows.rearrange("(p j) c -> p j c", j=PACK))
             return tile
 
+        def load_wb_half(a, b, half):
+            tile = sb("wb_raw%d%d_%d" % (a, b, half), [P, PACK, KP // 2], F32)
+            c0 = KP * b + KP // 2 * half
+            rows = wb[KP * a : KP * (a + 1), c0 : c0 + KP // 2]
+            nc.sync.dma_start(out=tile[:], in_=rows.rearrange("(p j) c -> p j c", j=PACK))
+            return tile
+
         def load_wa(b, tag=""):
             tile = sb("wa_raw%d" % b, [P, 2, KP // 2], I32, tag)
             cols = wa_words[:, :, 2 * KP * b : 2 * KP * (b + 1)]
             nc.sync.dma_start(out=tile[:], in_=cols.rearrange("a p n -> p a n").bitcast(I32))
             return tile
 
+        wa_raw = [load_wa(0)]
         load_rows(tab_s, tab_scales)
         nc.sync.dma_start(out=offs_t[:], in_=offs)
-        wa_raw = [load_wa(0)]
         load_side_by_side(wa_s_raw, wa_scales, 0)
         tab_w = [load_words("tab_w0", tab_words[0])]
         tab_w.append(load_words("tab_w1", tab_words[1]))
@@ -105,15 +112,6 @@ def tile_list_airway_series_conductance_kernel(
             tile = sb(name, [P, count], dtype, tag)
             nc.vector.tensor_copy(out=tile[:], in_=window.indirect(offsets))
             return tile
-
-        v_s0 = gather("v_s0", tab_s[:], offs_t[:], S, U8)
-        move_rows(v_s, v_s0, 0)
-        wa_raw.append(load_wa(1, "late"))
-        wb_raw = {(0, 0): load_wb(0, 0)}
-        load_rows(tab2_s, tab2_scales)
-        nc.sync.dma_start(out=offs2_t[:], in_=offs2)
-        tab2_w = [load_words("tab2_w%d" % a, tab2_words[a]) for a in range(2)]
-        wb_raw[1, 0] = load_wb(1, 0)
 
         def deal_wa(b):
             tile = sb("wa_w%d" % b, [P, 2, 2 * KP], U8)
@@ -125,22 +123,40 @@ def tile_list_airway_series_conductance_kernel(
             )
             return tile
 
+        def pool_deal_wa(b):
+            tile = sb("wa_w%d" % b, [P, 2, 2 * KP], U8)
+            nc.gpsimd.tensor_copy(
+                out=tile[:].rearrange("p a (t m e) -> p a t m e", t=PACK, e=2),
+                in_=wa_raw[b][:].rearrange("p a n -> p (a n)").bitcast(U8).rearrange(
+                    "p (a m t e) -> p a t m e", a=2, t=PACK, e=2),
+            )
+            return tile
+
+        wa_w = [deal_wa(0)]
+        v_s0 = gather("v_s0", tab_s[:], offs_t[:], S, U8)
+        move_rows(v_s, v_s0, 0)
+        wa_raw.append(load_wa(1))
+        wb_raw = {(0, 0): load_wb(0, 0)}
+        load_rows(tab2_s, tab2_scales)
+        nc.sync.dma_start(out=offs2_t[:], in_=offs2)
+        tab2_w = [load_words("tab2_w%d" % a, tab2_words[a]) for a in range(2)]
+        wb_raw[1, 0] = load_wb(1, 0)
+
         v_w = {}
 
         def gather_tab(a, h, tag=""):
             v_w[a, h] = gather("v_w%d%d" % (a, h), tab_w[a][:].bitcast(U32),
                                offs_t[:, 32 * h : 32 * (h + 1)], BANK, U32, tag)
 
-        wa_w = [deal_wa(0)]
         gather_tab(0, 0)
         wa_s = sb("wa_s", [P, 2, H], U8)
-        nc.vector.tensor_copy(
-            out=wa_s[:].rearrange("p a (b t c i) -> p (a b) c t i", t=PACK, c=8, i=16),
-            in_=wa_s_raw[:].rearrange("p a (b c i t) -> p (a b) c t i", t=PACK, c=8, i=16),
+        nc.gpsimd.tensor_copy(
+            out=wa_s[:].rearrange("p a (b t m) -> p (a b) t m", t=PACK, m=P),
+            in_=wa_s_raw[:].rearrange("p a (b m t) -> p (a b) t m", t=PACK, m=P),
         )
         gather_tab(0, 1)
         gather_tab(1, 0)
-        wa_w.append(deal_wa(1))
+        wa_w.append(pool_deal_wa(1))
         gather_tab(1, 1)
         v2_s0 = gather("v2_s0", tab2_s[:], offs2_t[:], M, U8)
         move_rows(v2_s, v2_s0, 4)
@@ -148,7 +164,7 @@ def tile_list_airway_series_conductance_kernel(
         nc.sync.dma_start(out=pos_t[:], in_=pos1)
         drive_t = sb("drive_t", [P, 2, PACK], F32)
         nc.sync.dma_start(out=drive_t[:], in_=drive.rearrange("(b p t) -> p b t", p=P, t=PACK))
-        wb_raw[1, 1] = load_wb(1, 1)
+        last_raw = [load_wb_half(1, 1, half) for half in range(2)]
         wf_w = load_both_passes("wf_w", wf_words, "")
         load_side_by_side(wf_s, wf_scales, 8)
 
@@ -172,11 +188,18 @@ def tile_list_airway_series_conductance_kernel(
                 nc.gpsimd.tensor_copy(out=out[:, rows].rearrange("p m j t -> p m t j"),
                                       in_=in_[:, rows].rearrange("p m j t -> p m t j"))
 
-        first = cast_wb(0, 0, pool_copy, "late")
+        first = cast_wb(0, 0, pool_copy)
         v2_w = [gather("v2_w%d" % a, tab2_w[a][:].bitcast(U32), offs2_t[:], M, U32) for a in range(2)]
         wb_q = {(0, 0): quantize("wb_q00", first[:], KP, "tab2_w1")}
-        for a, b in ((1, 0), (0, 1), (1, 1)):
+        for a, b in ((1, 0), (0, 1)):
             wb_q[a, b] = quantize("wb_q%d%d" % (a, b), cast_wb(a, b, nc.vector.tensor_copy)[:], KP)
+        last_bf = sb("wb_bf11", [P, KP * PACK], BF16)
+        for half in range(2):
+            nc.vector.tensor_copy(
+                out=last_bf[:].rearrange("p (t m j) -> p m j t", t=PACK, j=PACK)[:, 64 * half : 64 * (half + 1)],
+                in_=last_raw[half][:].rearrange("p j (m t) -> p m j t", t=PACK),
+            )
+        wb_q[1, 1] = quantize("wb_q11", last_bf[:], KP)
 
         ra = {(b, t): sb("ra%d%d" % (b, t), [P, S], F32) for b in range(2) for t in range(PACK)}
         rb = {(b, t): sb("rb%d%d" % (b, t), [P, M], F32) for b in range(2) for t in range(PACK)}
@@ -254,7 +277,7 @@ def tile_list_airway_series_conductance_kernel(
                 nc.scalar.activation(out=dst, in_=src, func=ACT.Square)
             return quantize("z_q%d_%d" % (b, c0), z_bf[:], width)
 
-        series0 = make_series(0, 0, M, "wb_raw11")
+        series0 = make_series(0, 0, M, "wb_raw11_1")
         series = {(0, h): series0[:, :, HALF * h : HALF * (h + 1)] for h in range(2)}
         for h in range(2):
             series[1, h] = make_series(1, HALF * h, HALF)[:]
@@ -278,7 +301,11 @@ def tile_list_airway_series_conductance_kernel(
             for pair in range(2):
                 res = sb("res%d%d" % (h, pair), [P, 2, HALF], F32)
                 copies = (nc.scalar.copy if h == 0 else nc.vector.tensor_copy, nc.scalar.copy)
+                rows = out[2 * P * pair : 2 * P * (pair + 1), HALF * h : HALF * (h + 1)]
+                rows = rows.rearrange("(j p) m -> p j m", p=P)
                 for i, engine_copy in enumerate(copies):
                     engine_copy(out=res[:, i, :], in_=accs[2 * pair + i][:])
-                rows = out[2 * P * pair : 2 * P * (pair + 1), HALF * h : HALF * (h + 1)]
-                nc.sync.dma_start(out=rows.rearrange("(j p) m -> p j m", p=P), in_=res[:])
+                    if h == 1:
+                        nc.sync.dma_start(out=rows[:, i, :], in_=res[:, i, :])
+                if h == 0:
+                    nc.sync.dma_start(out=rows, in_=res[:])

@@ -56,10 +56,10 @@ def tile_list_airway_series_conductance_kernel(
         nc.gpsimd.memset(wf_s[:].rearrange("p a n -> p (a n)").bitcast(I32), 0)
 
         def load_side_by_side(plane, scales, first):
-            for q in range(4):
+            for r in range(4):
                 nc.sync.dma_start(
-                    out=plane[32 * q + first : 32 * q + first + 4, :, :].bitcast(I32),
-                    in_=scales[:, 4 * q : 4 * q + 4, :].rearrange("a r n -> r a n").bitcast(I32),
+                    out=plane[first + r : P : 32, :, :].bitcast(I32),
+                    in_=scales[:, r:16:4, :].rearrange("a q n -> q a n").bitcast(I32),
                 )
 
         def load_rows(window, scales):
@@ -67,7 +67,7 @@ def tile_list_airway_series_conductance_kernel(
                               in_=scales.rearrange("a q n -> q a n").bitcast(I32))
 
         def move_rows(plane, rows, first):
-            for q in range(4):
+            for q in (0, 2, 1, 3):
                 nc.sync.dma_start(
                     out=plane[32 * q + first : 32 * q + first + 4, :, :].rearrange("p a n -> p (a n)").bitcast(I32),
                     in_=rows[96 + 8 * q : 104 + 8 * q, :].bitcast(I32))
@@ -123,19 +123,10 @@ def tile_list_airway_series_conductance_kernel(
             )
             return tile
 
-        def pool_deal_wa(b):
-            tile = sb("wa_w%d" % b, [P, 2, 2 * KP], U8)
-            nc.gpsimd.tensor_copy(
-                out=tile[:].rearrange("p a (t m e) -> p a t m e", t=PACK, e=2),
-                in_=wa_raw[b][:].rearrange("p a n -> p (a n)").bitcast(U8).rearrange(
-                    "p (a m t e) -> p a t m e", a=2, t=PACK, e=2),
-            )
-            return tile
-
         wa_w = [deal_wa(0)]
         v_s0 = gather("v_s0", tab_s[:], offs_t[:], S, U8)
         move_rows(v_s, v_s0, 0)
-        wa_raw.append(load_wa(1))
+        wa_raw.append(load_wa(1, "late"))
         wb_raw = {(0, 0): load_wb(0, 0)}
         load_rows(tab2_s, tab2_scales)
         nc.sync.dma_start(out=offs2_t[:], in_=offs2)
@@ -156,7 +147,7 @@ def tile_list_airway_series_conductance_kernel(
         )
         gather_tab(0, 1)
         gather_tab(1, 0)
-        wa_w.append(pool_deal_wa(1))
+        wa_w.append(deal_wa(1))
         gather_tab(1, 1)
         v2_s0 = gather("v2_s0", tab2_s[:], offs2_t[:], M, U8)
         move_rows(v2_s, v2_s0, 4)
@@ -188,21 +179,22 @@ def tile_list_airway_series_conductance_kernel(
                 nc.gpsimd.tensor_copy(out=out[:, rows].rearrange("p m j t -> p m t j"),
                                       in_=in_[:, rows].rearrange("p m j t -> p m t j"))
 
-        first = cast_wb(0, 0, pool_copy)
+        first = cast_wb(0, 0, pool_copy, "late")
         v2_w = [gather("v2_w%d" % a, tab2_w[a][:].bitcast(U32), offs2_t[:], M, U32) for a in range(2)]
         wb_q = {(0, 0): quantize("wb_q00", first[:], KP, "tab2_w1")}
         for a, b in ((1, 0), (0, 1)):
             wb_q[a, b] = quantize("wb_q%d%d" % (a, b), cast_wb(a, b, nc.vector.tensor_copy)[:], KP)
         last_bf = sb("wb_bf11", [P, KP * PACK], BF16)
-        for half in range(2):
-            nc.vector.tensor_copy(
+        for half, engine_copy in enumerate((nc.scalar.copy, nc.vector.tensor_copy)):
+            engine_copy(
                 out=last_bf[:].rearrange("p (t m j) -> p m j t", t=PACK, j=PACK)[:, 64 * half : 64 * (half + 1)],
                 in_=last_raw[half][:].rearrange("p j (m t) -> p m j t", t=PACK),
             )
-        wb_q[1, 1] = quantize("wb_q11", last_bf[:], KP)
+        last_q = [quantize("wb_q11_%d" % pair, last_bf[:, 2 * KP * pair : 2 * KP * (pair + 1)], KP // 2)
+                  for pair in range(2)]
 
         ra = {(b, t): sb("ra%d%d" % (b, t), [P, S], F32) for b in range(2) for t in range(PACK)}
-        rb = {(b, t): sb("rb%d%d" % (b, t), [P, M], F32) for b in range(2) for t in range(PACK)}
+        rb = [sb("rb_%d" % b, [P, PACK, M], F32, tag) for b, tag in enumerate(("wb_raw11_0", ""))]
 
         def make_ra(b, t, h, index):
             c0 = KP * b + P * t
@@ -223,7 +215,11 @@ def tile_list_airway_series_conductance_kernel(
             acc = bank([P, BANK], (PACK * b + t + 4) % 8)
             cols = slice(P * t, P * (t + 1))
             for a in range(2):
-                codes, scales = wb_q[a, b]
+                if (a, b) == (1, 1):
+                    codes, scales = last_q[t // 2]
+                    cols = slice(P * (t % 2), P * (t % 2 + 1))
+                else:
+                    codes, scales = wb_q[a, b]
                 nc.tensor.matmul_mx(
                     out=acc[:],
                     lhsT=codes[:, cols].bitcast(FP8X4),
@@ -232,7 +228,7 @@ def tile_list_airway_series_conductance_kernel(
                     rhs_scale=v2_s[4:P, a, :],
                     start=(a == 0), stop=(a == 1),
                 )
-            nc.scalar.activation(out=rb[b, t][:], in_=acc[:], func=ACT.Exp, scale=-1.0)
+            nc.scalar.activation(out=rb[b][:, t, :], in_=acc[:], func=ACT.Exp, scale=-1.0)
 
         for b in range(2):
             for h in range(2):
@@ -242,7 +238,7 @@ def tile_list_airway_series_conductance_kernel(
             for t in range(PACK):
                 make_rb(b, t)
 
-        inv_drive = sb("inv_drive", [P, 2 * PACK], F32, "wb_q11_s")
+        inv_drive = sb("inv_drive", [P, 2 * PACK], F32, "wb_q11_1_s")
         nc.vector.reciprocal(out=inv_drive[:], in_=drive_t[:].rearrange("p b t -> p (b t)"))
 
         def make_series(b, c0, width, tag=""):
@@ -251,7 +247,7 @@ def tile_list_airway_series_conductance_kernel(
                 nc.vector.tensor_tensor(
                     out=tile[:, t, :],
                     in0=ra[b, t][:].indirect(pos_t[:, c0 // 16 : (c0 + width) // 16]),
-                    in1=rb[b, t][:, c0 : c0 + width],
+                    in1=rb[b][:, t, c0 : c0 + width],
                     op=ALU.add,
                 )
             return tile

@@ -48,12 +48,12 @@ def tile_list_airway_series_conductance_kernel(
         v2_s = sb("v2_s", [P, 2, M], U8)
         wf_s = sb("wf_s", [P, 2, N], U8)
         v_s = sb("v_s", [P, 2, S], U8)
-        nc.vector.memset(tab_s[0:96, :].bitcast(I32), 0)
         nc.gpsimd.memset(wa_s_raw[:].rearrange("p a n -> p (a n)").bitcast(I32), 0)
-        nc.gpsimd.memset(v_s[:].rearrange("p a n -> p (a n)").bitcast(I32), 0)
-        nc.gpsimd.memset(tab2_s[0:96, :].bitcast(I32), 0)
-        nc.gpsimd.memset(v2_s[:].rearrange("p a n -> p (a n)").bitcast(I32), 0)
-        nc.gpsimd.memset(wf_s[:].rearrange("p a n -> p (a n)").bitcast(I32), 0)
+        nc.vector.memset(tab_s[0:96, :].bitcast(I32), 0)
+        nc.vector.memset(v_s[:].rearrange("p a n -> p (a n)").bitcast(I32), 0)
+        nc.vector.memset(tab2_s[0:96, :].bitcast(I32), 0)
+        nc.vector.memset(v2_s[:].rearrange("p a n -> p (a n)").bitcast(I32), 0)
+        nc.vector.memset(wf_s[:].rearrange("p a n -> p (a n)").bitcast(I32), 0)
 
         def load_side_by_side(plane, scales, first):
             for r in range(4):
@@ -104,8 +104,8 @@ def tile_list_airway_series_conductance_kernel(
         wa_raw = [load_wa(0)]
         load_rows(tab_s, tab_scales)
         nc.sync.dma_start(out=offs_t[:], in_=offs)
-        load_side_by_side(wa_s_raw, wa_scales, 0)
         tab_w = [load_words("tab_w0", tab_words[0])]
+        load_side_by_side(wa_s_raw, wa_scales, 0)
         tab_w.append(load_words("tab_w1", tab_words[1]))
 
         def gather(name, window, offsets, count, dtype, tag=""):
@@ -140,11 +140,13 @@ def tile_list_airway_series_conductance_kernel(
                                offs_t[:, 32 * h : 32 * (h + 1)], BANK, U32, tag)
 
         gather_tab(0, 0)
-        wa_s = sb("wa_s", [P, 2, H], U8)
-        nc.gpsimd.tensor_copy(
-            out=wa_s[:].rearrange("p a (b t m) -> p (a b) t m", t=PACK, m=P),
-            in_=wa_s_raw[:].rearrange("p a (b m t) -> p (a b) t m", t=PACK, m=P),
-        )
+        wa_s = []
+        for b in range(2):
+            wa_s.append(sb("wa_s%d" % b, [P, 2, KP], U8))
+            nc.gpsimd.tensor_copy(
+                out=wa_s[b][:].rearrange("p a (t m) -> p a t m", t=PACK),
+                in_=wa_s_raw[:, :, KP * b : KP * (b + 1)].rearrange("p a (m t) -> p a t m", t=PACK),
+            )
         gather_tab(0, 1)
         gather_tab(1, 0)
         wa_w.append(deal_wa(1))
@@ -153,9 +155,9 @@ def tile_list_airway_series_conductance_kernel(
         move_rows(v2_s, v2_s0, 4)
         wb_raw[0, 1] = load_wb(0, 1)
         nc.sync.dma_start(out=pos_t[:], in_=pos1)
+        last_raw = [load_wb_half(1, 1, half) for half in range(2)]
         drive_t = sb("drive_t", [P, 2, PACK], F32)
         nc.sync.dma_start(out=drive_t[:], in_=drive.rearrange("(b p t) -> p b t", p=P, t=PACK))
-        last_raw = [load_wb_half(1, 1, half) for half in range(2)]
         wf_w = load_both_passes("wf_w", wf_words, "")
         load_side_by_side(wf_s, wf_scales, 8)
 
@@ -197,14 +199,13 @@ def tile_list_airway_series_conductance_kernel(
         rb = [sb("rb_%d" % b, [P, PACK, M], F32, tag) for b, tag in enumerate(("wb_raw11_0", ""))]
 
         def make_ra(b, t, h, index):
-            c0 = KP * b + P * t
             cols = slice(BANK * h, BANK * (h + 1))
             acc = bank([P, BANK], index)
             for a in range(2):
                 nc.tensor.matmul_mx(
                     out=acc[:],
                     lhsT=wa_w[b][:, a, 2 * P * t : 2 * P * (t + 1)].bitcast(FP4X4),
-                    lhsT_scale=wa_s[:, a, c0 : c0 + P],
+                    lhsT_scale=wa_s[b][:, a, P * t : P * (t + 1)],
                     rhs=v_w[a, h][:].bitcast(FP8X4),
                     rhs_scale=v_s[:, a, cols],
                     start=(a == 0), stop=(a == 1),
@@ -296,7 +297,7 @@ def tile_list_airway_series_conductance_kernel(
         for h, accs in enumerate(results):
             for pair in range(2):
                 res = sb("res%d%d" % (h, pair), [P, 2, HALF], F32)
-                copies = (nc.scalar.copy if h == 0 else nc.vector.tensor_copy, nc.scalar.copy)
+                copies = (nc.vector.tensor_copy, nc.scalar.copy)
                 rows = out[2 * P * pair : 2 * P * (pair + 1), HALF * h : HALF * (h + 1)]
                 rows = rows.rearrange("(j p) m -> p j m", p=P)
                 for i, engine_copy in enumerate(copies):

@@ -293,6 +293,17 @@ def tile_list_airway_series_conductance_kernel(
                         rhs_scale=scales[:],
                         start=(b == 0), stop=(b == 1),
                     )
+                if (b, h) == (0, 0):
+                    idle = bank([P, HALF], 7)
+                    for j in range(3):
+                        nc.tensor.matmul_mx(
+                            out=idle[:],
+                            lhsT=wf_w[:, 0, P * j : P * (j + 1)].bitcast(FP8X4),
+                            lhsT_scale=wf_s[8:P, 0, P * j : P * (j + 1)],
+                            rhs=codes[:].bitcast(FP8X4),
+                            rhs_scale=scales[:],
+                            start=True, stop=True,
+                        )
             results.append(accs)
         for h, accs in enumerate(results):
             for pair in range(2):

@@ -154,8 +154,8 @@ def tile_list_airway_series_conductance_kernel(
         v2_s0 = gather("v2_s0", tab2_s[:], offs2_t[:], M, U8)
         move_rows(v2_s, v2_s0, 4)
         wb_raw[0, 1] = load_wb(0, 1)
-        nc.sync.dma_start(out=pos_t[:], in_=pos1)
         last_raw = [load_wb_half(1, 1, half) for half in range(2)]
+        nc.sync.dma_start(out=pos_t[:], in_=pos1)
         drive_t = sb("drive_t", [P, 2, PACK], F32)
         nc.sync.dma_start(out=drive_t[:], in_=drive.rearrange("(b p t) -> p b t", p=P, t=PACK))
         wf_w = load_both_passes("wf_w", wf_words, "")
@@ -295,7 +295,7 @@ def tile_list_airway_series_conductance_kernel(
                     )
                 if (b, h) == (0, 0):
                     idle = bank([P, HALF], 7)
-                    for j in range(3):
+                    for j in (0, 1, 2, 3, 0):
                         nc.tensor.matmul_mx(
                             out=idle[:],
                             lhsT=wf_w[:, 0, P * j : P * (j + 1)].bitcast(FP8X4),

@@ -21,6 +21,9 @@ PACK = 4
 KP = P * PACK
 BANK = 512
 HALF = M // 2
+FIRST_BANKS = 6
+LAST_ON_VECTOR = 128
+HEAD_WARM = 3
 
 
 def tile_list_airway_series_conductance_kernel(
@@ -101,10 +104,10 @@ def tile_list_airway_series_conductance_kernel(
             nc.sync.dma_start(out=tile[:], in_=cols.rearrange("a p n -> p a n").bitcast(I32))
             return tile
 
-        wa_raw = [load_wa(0)]
-        load_rows(tab_s, tab_scales)
         nc.sync.dma_start(out=offs_t[:], in_=offs)
+        load_rows(tab_s, tab_scales)
         tab_w = [load_words("tab_w0", tab_words[0])]
+        wa_raw = [load_wa(0)]
         load_side_by_side(wa_s_raw, wa_scales, 0)
         tab_w.append(load_words("tab_w1", tab_words[1]))
 
@@ -113,9 +116,9 @@ def tile_list_airway_series_conductance_kernel(
             nc.vector.tensor_copy(out=tile[:], in_=window.indirect(offsets))
             return tile
 
-        def deal_wa(b):
+        def deal_wa(b, engine_copy):
             tile = sb("wa_w%d" % b, [P, 2, 2 * KP], U8)
-            nc.vector.tensor_copy(
+            engine_copy(
                 out=tile[:].rearrange("p a n -> p (a n)").bitcast(U16).rearrange(
                     "p (a t c i) -> p a c t i", t=PACK, c=16, i=8),
                 in_=wa_raw[b][:].rearrange("p a n -> p (a n)").bitcast(U16).rearrange(
@@ -123,7 +126,7 @@ def tile_list_airway_series_conductance_kernel(
             )
             return tile
 
-        wa_w = [deal_wa(0)]
+        wa_w = [deal_wa(0, nc.scalar.copy)]
         v_s0 = gather("v_s0", tab_s[:], offs_t[:], S, U8)
         move_rows(v_s, v_s0, 0)
         wa_raw.append(load_wa(1, "late"))
@@ -133,13 +136,14 @@ def tile_list_airway_series_conductance_kernel(
         tab2_w = [load_words("tab2_w%d" % a, tab2_words[a]) for a in range(2)]
         wb_raw[1, 0] = load_wb(1, 0)
 
-        v_w = {}
+        v_w = [sb("v_w%d" % a, [P, S], U32) for a in range(2)]
 
-        def gather_tab(a, h, tag=""):
-            v_w[a, h] = gather("v_w%d%d" % (a, h), tab_w[a][:].bitcast(U32),
-                               offs_t[:, 32 * h : 32 * (h + 1)], BANK, U32, tag)
+        def gather_tab(a, c0, c1):
+            nc.vector.tensor_copy(out=v_w[a][:, c0:c1],
+                                  in_=tab_w[a][:].bitcast(U32).indirect(offs_t[:, c0 // 16 : c1 // 16]))
 
-        gather_tab(0, 0)
+        first_chunks = ((0, 256), (256, 512), (512, 1024))
+        later_chunks = ((0, 512), (512, 1024))
         wa_s = []
         for b in range(2):
             wa_s.append(sb("wa_s%d" % b, [P, 2, KP], U8))
@@ -147,10 +151,11 @@ def tile_list_airway_series_conductance_kernel(
                 out=wa_s[b][:].rearrange("p a (t m) -> p a t m", t=PACK),
                 in_=wa_s_raw[:, :, KP * b : KP * (b + 1)].rearrange("p a (m t) -> p a t m", t=PACK),
             )
-        gather_tab(0, 1)
-        gather_tab(1, 0)
-        wa_w.append(deal_wa(1))
-        gather_tab(1, 1)
+        for c0, c1 in later_chunks:
+            gather_tab(0, c0, c1)
+        for c0, c1 in first_chunks:
+            gather_tab(1, c0, c1)
+        wa_w.append(deal_wa(1, nc.vector.tensor_copy))
         v2_s0 = gather("v2_s0", tab2_s[:], offs2_t[:], M, U8)
         move_rows(v2_s, v2_s0, 4)
         wb_raw[0, 1] = load_wb(0, 1)
@@ -198,22 +203,21 @@ def tile_list_airway_series_conductance_kernel(
         ra = {(b, t): sb("ra%d%d" % (b, t), [P, S], F32) for b in range(2) for t in range(PACK)}
         rb = [sb("rb_%d" % b, [P, PACK, M], F32, tag) for b, tag in enumerate(("wb_raw11_0", ""))]
 
-        def make_ra(b, t, h, index):
-            cols = slice(BANK * h, BANK * (h + 1))
-            acc = bank([P, BANK], index)
+        def make_ra(b, t, c0, c1, index):
+            acc = bank([P, c1 - c0], index)
             for a in range(2):
                 nc.tensor.matmul_mx(
                     out=acc[:],
                     lhsT=wa_w[b][:, a, 2 * P * t : 2 * P * (t + 1)].bitcast(FP4X4),
                     lhsT_scale=wa_s[b][:, a, P * t : P * (t + 1)],
-                    rhs=v_w[a, h][:].bitcast(FP8X4),
-                    rhs_scale=v_s[:, a, cols],
+                    rhs=v_w[a][:, c0:c1].bitcast(FP8X4),
+                    rhs_scale=v_s[:, a, c0:c1],
                     start=(a == 0), stop=(a == 1),
                 )
-            nc.scalar.activation(out=ra[b, t][:, cols], in_=acc[:], func=ACT.Exp, scale=-1.0)
+            nc.scalar.activation(out=ra[b, t][:, c0:c1], in_=acc[:], func=ACT.Exp, scale=-1.0)
 
-        def make_rb(b, t):
-            acc = bank([P, BANK], (PACK * b + t + 4) % 8)
+        def make_rb(b, t, index):
+            acc = bank([P, BANK], index)
             cols = slice(P * t, P * (t + 1))
             for a in range(2):
                 if (a, b) == (1, 1):
@@ -231,89 +235,90 @@ def tile_list_airway_series_conductance_kernel(
                 )
             nc.scalar.activation(out=rb[b][:, t, :], in_=acc[:], func=ACT.Exp, scale=-1.0)
 
-        for b in range(2):
-            for h in range(2):
-                for t in range(PACK):
-                    make_ra(b, t, h, (8 * b + PACK * h + t) % 6)
+        idle = bank([P, BANK], 7)
+        for t in range(HEAD_WARM):
+            nc.tensor.matmul_mx(
+                out=idle[:],
+                lhsT=wa_raw[0][:, 0, P // 2 * t : P // 2 * (t + 1)].bitcast(FP4X4),
+                lhsT_scale=wa_s_raw[:, 0, P * t : P * (t + 1)],
+                rhs=v_w[0][:, 0:BANK].bitcast(FP8X4),
+                rhs_scale=wa_s_raw[:, 0, 0:BANK],
+                start=True, stop=True,
+            )
+        pieces = [(b, t, c0, c1) for b, chunks in enumerate((first_chunks, later_chunks))
+                  for c0, c1 in chunks for t in range(PACK)]
+        for n, piece in enumerate(pieces):
+            make_ra(*piece, n % FIRST_BANKS)
         for b in range(2):
             for t in range(PACK):
-                make_rb(b, t)
+                make_rb(b, t, (len(pieces) + PACK * b + t) % FIRST_BANKS)
 
         inv_drive = sb("inv_drive", [P, 2 * PACK], F32, "wb_q11_1_s")
         nc.vector.reciprocal(out=inv_drive[:], in_=drive_t[:].rearrange("p b t -> p (b t)"))
 
-        def make_series(b, c0, width, tag=""):
-            tile = sb("series%d_%d" % (b, c0), [P, PACK, width], F32, tag)
-            for t in range(PACK):
-                nc.vector.tensor_tensor(
-                    out=tile[:, t, :],
-                    in0=ra[b, t][:].indirect(pos_t[:, c0 // 16 : (c0 + width) // 16]),
-                    in1=rb[b][:, t, c0 : c0 + width],
-                    op=ALU.add,
-                )
-            return tile
+        def make_series(b, c0, width, tags):
+            rows = []
+            for pair, tag in enumerate(tags):
+                tile = sb("series%d_%d_%d" % (b, c0, pair), [P, 2, width], F32, tag)
+                for t in range(2 * pair, 2 * pair + 2):
+                    nc.vector.tensor_tensor(
+                        out=tile[:, t % 2, :],
+                        in0=ra[b, t][:].indirect(pos_t[:, c0 // 16 : (c0 + width) // 16]),
+                        in1=rb[b][:, t, c0 : c0 + width],
+                        op=ALU.add,
+                    )
+                    rows.append(tile[:, t % 2, :])
+            return rows
 
-        def make_root(b, c0, series, tag=""):
-            root = sb("root%d_%d" % (b, c0), [P, PACK, HALF], F32, tag)
+        def make_root(b, h, rows):
+            root = sb("root%d_%d" % (b, h), [P, PACK, HALF], F32)
             for t in range(PACK):
                 s = PACK * b + t
                 nc.scalar.activation(
-                    out=root[:, t, :], in_=series[:, t, :],
+                    out=root[:, t, :], in_=rows[t],
                     func=ACT.Abs_reciprocal_sqrt, scale=inv_drive[:, s : s + 1],
                 )
             return root
 
-        def make_z(b, c0, root, on_vector):
-            width = root.shape[2]
-            z_bf = sb("z_bf%d_%d" % (b, c0), [P, width * PACK], BF16)
-            dst = z_bf[:].rearrange("p (c i t) -> p c t i", i=4, t=PACK)
-            src = root[:].rearrange("p t (c i) -> p c t i", i=4)
+        accs = [[bank([P, HALF], PACK * h + j) for j in range(4)] for h in range(2)]
+
+        def square(z_bf, root, c0, c1, on_vector):
+            dst = z_bf[:, PACK * c0 : PACK * c1].rearrange("p (c i t) -> p c t i", i=4, t=PACK)
+            src = root[:, :, c0:c1].rearrange("p t (c i) -> p c t i", i=4)
             if on_vector:
                 nc.vector.tensor_tensor(out=dst, in0=src, in1=src, op=ALU.mult)
             else:
                 nc.scalar.activation(out=dst, in_=src, func=ACT.Square)
-            return quantize("z_q%d_%d" % (b, c0), z_bf[:], width)
 
-        series0 = make_series(0, 0, M, "wb_raw11_1")
-        series = {(0, h): series0[:, :, HALF * h : HALF * (h + 1)] for h in range(2)}
+        def multiply_unit(b, h, root, vector_cols):
+            z_bf = sb("z_bf%d_%d" % (b, h), [P, HALF * PACK], BF16)
+            if vector_cols > 0:
+                square(z_bf, root, 0, vector_cols, True)
+            if vector_cols < HALF:
+                square(z_bf, root, vector_cols, HALF, False)
+            codes, scales = quantize("z_q%d_%d" % (b, h), z_bf[:], HALF)
+            for j in range(4):
+                ncols = slice(P * j, P * (j + 1))
+                nc.tensor.matmul_mx(
+                    out=accs[h][j][:],
+                    lhsT=wf_w[:, b, ncols].bitcast(FP8X4),
+                    lhsT_scale=wf_s[8:P, b, ncols],
+                    rhs=codes[:].bitcast(FP8X4),
+                    rhs_scale=scales[:],
+                    start=(b == 0), stop=(b == 1),
+                )
+
+        series0 = make_series(0, 0, M, ("wb_bf11", ""))
+        first_half = make_series(1, 0, HALF, ("", ""))
+        multiply_unit(0, 0, make_root(0, 0, [row[:, 0:HALF] for row in series0])[:], 0)
+        second_half = make_series(1, HALF, HALF, ("", "z_bf0_0"))
+        root01 = make_root(0, 1, [row[:, HALF:M] for row in series0])
+        multiply_unit(1, 0, make_root(1, 0, first_half)[:], HALF)
+        multiply_unit(0, 1, root01[:], 0)
+        multiply_unit(1, 1, make_root(1, 1, second_half)[:], LAST_ON_VECTOR)
         for h in range(2):
-            series[1, h] = make_series(1, HALF * h, HALF)[:]
-        results = []
-        for h in range(2):
-            accs = [bank([P, HALF], PACK * h + j) for j in range(4)]
-            for b in range(2):
-                codes, scales = make_z(b, h, make_root(b, h, series[b, h]), on_vector=(b != h))
-                for j in range(4):
-                    ncols = slice(P * j, P * (j + 1))
-                    nc.tensor.matmul_mx(
-                        out=accs[j][:],
-                        lhsT=wf_w[:, b, ncols].bitcast(FP8X4),
-                        lhsT_scale=wf_s[8:P, b, ncols],
-                        rhs=codes[:].bitcast(FP8X4),
-                        rhs_scale=scales[:],
-                        start=(b == 0), stop=(b == 1),
-                    )
-                if (b, h) == (0, 0):
-                    idle = bank([P, HALF], 7)
-                    for j in (0, 1, 2, 3, 0):
-                        nc.tensor.matmul_mx(
-                            out=idle[:],
-                            lhsT=wf_w[:, 0, P * j : P * (j + 1)].bitcast(FP8X4),
-                            lhsT_scale=wf_s[8:P, 0, P * j : P * (j + 1)],
-                            rhs=codes[:].bitcast(FP8X4),
-                            rhs_scale=scales[:],
-                            start=True, stop=True,
-                        )
-            results.append(accs)
-        for h, accs in enumerate(results):
-            for pair in range(2):
-                res = sb("res%d%d" % (h, pair), [P, 2, HALF], F32)
-                copies = (nc.vector.tensor_copy, nc.scalar.copy)
-                rows = out[2 * P * pair : 2 * P * (pair + 1), HALF * h : HALF * (h + 1)]
-                rows = rows.rearrange("(j p) m -> p j m", p=P)
-                for i, engine_copy in enumerate(copies):
-                    engine_copy(out=res[:, i, :], in_=accs[2 * pair + i][:])
-                    if h == 1:
-                        nc.sync.dma_start(out=rows[:, i, :], in_=res[:, i, :])
-                if h == 0:
-                    nc.sync.dma_start(out=rows, in_=res[:])
+            for j in range(4):
+                res = sb("res%d%d" % (h, j), [P, HALF], F32)
+                engine_copy = nc.vector.tensor_copy if h == 1 and j < 3 else nc.scalar.copy
+                engine_copy(out=res[:], in_=accs[h][j][:])
+                nc.sync.dma_start(out=out[P * j : P * (j + 1), HALF * h : HALF * (h + 1)], in_=res[:])

@@ -22,7 +22,6 @@ KP = P * PACK
 BANK = 512
 HALF = M // 2
 FIRST_BANKS = 6
-LAST_ON_VECTOR = 128
 HEAD_WARM = 3
 
 
@@ -256,69 +255,78 @@ def tile_list_airway_series_conductance_kernel(
         inv_drive = sb("inv_drive", [P, 2 * PACK], F32, "wb_q11_1_s")
         nc.vector.reciprocal(out=inv_drive[:], in_=drive_t[:].rearrange("p b t -> p (b t)"))
 
-        def make_series(b, c0, width, tags):
-            rows = []
-            for pair, tag in enumerate(tags):
-                tile = sb("series%d_%d_%d" % (b, c0, pair), [P, 2, width], F32, tag)
-                for t in range(2 * pair, 2 * pair + 2):
-                    nc.vector.tensor_tensor(
-                        out=tile[:, t % 2, :],
-                        in0=ra[b, t][:].indirect(pos_t[:, c0 // 16 : (c0 + width) // 16]),
-                        in1=rb[b][:, t, c0 : c0 + width],
-                        op=ALU.add,
-                    )
-                    rows.append(tile[:, t % 2, :])
-            return rows
+        def make_series(b, c0, width, tag=""):
+            tile = sb("series%d_%d" % (b, c0), [P, PACK, width], F32, tag)
+            for t in range(PACK):
+                nc.vector.tensor_tensor(
+                    out=tile[:, t, :],
+                    in0=ra[b, t][:].indirect(pos_t[:, c0 // 16 : (c0 + width) // 16]),
+                    in1=rb[b][:, t, c0 : c0 + width],
+                    op=ALU.add,
+                )
+            return tile
 
-        def make_root(b, h, rows):
-            root = sb("root%d_%d" % (b, h), [P, PACK, HALF], F32)
+        def make_root(b, c0, series, tag=""):
+            root = sb("root%d_%d" % (b, c0), [P, PACK, HALF], F32, tag)
             for t in range(PACK):
                 s = PACK * b + t
                 nc.scalar.activation(
-                    out=root[:, t, :], in_=rows[t],
+                    out=root[:, t, :], in_=series[:, t, :],
                     func=ACT.Abs_reciprocal_sqrt, scale=inv_drive[:, s : s + 1],
                 )
             return root
 
-        accs = [[bank([P, HALF], PACK * h + j) for j in range(4)] for h in range(2)]
-
-        def square(z_bf, root, c0, c1, on_vector):
-            dst = z_bf[:, PACK * c0 : PACK * c1].rearrange("p (c i t) -> p c t i", i=4, t=PACK)
-            src = root[:, :, c0:c1].rearrange("p t (c i) -> p c t i", i=4)
+        def make_z(b, c0, root, on_vector):
+            width = root.shape[2]
+            z_bf = sb("z_bf%d_%d" % (b, c0), [P, width * PACK], BF16)
+            dst = z_bf[:].rearrange("p (c i t) -> p c t i", i=4, t=PACK)
+            src = root[:].rearrange("p t (c i) -> p c t i", i=4)
             if on_vector:
                 nc.vector.tensor_tensor(out=dst, in0=src, in1=src, op=ALU.mult)
             else:
                 nc.scalar.activation(out=dst, in_=src, func=ACT.Square)
+            return quantize("z_q%d_%d" % (b, c0), z_bf[:], width)
 
-        def multiply_unit(b, h, root, vector_cols):
-            z_bf = sb("z_bf%d_%d" % (b, h), [P, HALF * PACK], BF16)
-            if vector_cols > 0:
-                square(z_bf, root, 0, vector_cols, True)
-            if vector_cols < HALF:
-                square(z_bf, root, vector_cols, HALF, False)
-            codes, scales = quantize("z_q%d_%d" % (b, h), z_bf[:], HALF)
-            for j in range(4):
-                ncols = slice(P * j, P * (j + 1))
-                nc.tensor.matmul_mx(
-                    out=accs[h][j][:],
-                    lhsT=wf_w[:, b, ncols].bitcast(FP8X4),
-                    lhsT_scale=wf_s[8:P, b, ncols],
-                    rhs=codes[:].bitcast(FP8X4),
-                    rhs_scale=scales[:],
-                    start=(b == 0), stop=(b == 1),
-                )
-
-        series0 = make_series(0, 0, M, ("wb_bf11", ""))
-        first_half = make_series(1, 0, HALF, ("", ""))
-        multiply_unit(0, 0, make_root(0, 0, [row[:, 0:HALF] for row in series0])[:], 0)
-        second_half = make_series(1, HALF, HALF, ("", "z_bf0_0"))
-        root01 = make_root(0, 1, [row[:, HALF:M] for row in series0])
-        multiply_unit(1, 0, make_root(1, 0, first_half)[:], HALF)
-        multiply_unit(0, 1, root01[:], 0)
-        multiply_unit(1, 1, make_root(1, 1, second_half)[:], LAST_ON_VECTOR)
+        series0 = make_series(0, 0, M, "wb_raw11_1")
+        series = {(0, h): series0[:, :, HALF * h : HALF * (h + 1)] for h in range(2)}
         for h in range(2):
-            for j in range(4):
-                res = sb("res%d%d" % (h, j), [P, HALF], F32)
-                engine_copy = nc.vector.tensor_copy if h == 1 and j < 3 else nc.scalar.copy
-                engine_copy(out=res[:], in_=accs[h][j][:])
-                nc.sync.dma_start(out=out[P * j : P * (j + 1), HALF * h : HALF * (h + 1)], in_=res[:])
+            series[1, h] = make_series(1, HALF * h, HALF)[:]
+        results = []
+        for h in range(2):
+            accs = [bank([P, HALF], PACK * h + j) for j in range(4)]
+            for b in range(2):
+                codes, scales = make_z(b, h, make_root(b, h, series[b, h]), on_vector=(b != h))
+                for j in range(4):
+                    ncols = slice(P * j, P * (j + 1))
+                    nc.tensor.matmul_mx(
+                        out=accs[j][:],
+                        lhsT=wf_w[:, b, ncols].bitcast(FP8X4),
+                        lhsT_scale=wf_s[8:P, b, ncols],
+                        rhs=codes[:].bitcast(FP8X4),
+                        rhs_scale=scales[:],
+                        start=(b == 0), stop=(b == 1),
+                    )
+                if (b, h) == (0, 0):
+                    idle = bank([P, HALF], 7)
+                    for j in (0, 1, 2, 3, 0):
+                        nc.tensor.matmul_mx(
+                            out=idle[:],
+                            lhsT=wf_w[:, 0, P * j : P * (j + 1)].bitcast(FP8X4),
+                            lhsT_scale=wf_s[8:P, 0, P * j : P * (j + 1)],
+                            rhs=codes[:].bitcast(FP8X4),
+                            rhs_scale=scales[:],
+                            start=True, stop=True,
+                        )
+            results.append(accs)
+        for h, accs in enumerate(results):
+            for pair in range(2):
+                res = sb("res%d%d" % (h, pair), [P, 2, HALF], F32)
+                copies = (nc.vector.tensor_copy, nc.scalar.copy)
+                rows = out[2 * P * pair : 2 * P * (pair + 1), HALF * h : HALF * (h + 1)]
+                rows = rows.rearrange("(j p) m -> p j m", p=P)
+                for i, engine_copy in enumerate(copies):
+                    engine_copy(out=res[:, i, :], in_=accs[2 * pair + i][:])
+                    if h == 1:
+                        nc.sync.dma_start(out=rows[:, i, :], in_=res[:, i, :])
+                if h == 0:
+                    nc.sync.dma_start(out=rows, in_=res[:])

@@ -22,7 +22,6 @@ KP = P * PACK
 BANK = 512
 HALF = M // 2
 FIRST_BANKS = 6
-HEAD_WARM = 3
 
 
 def tile_list_airway_series_conductance_kernel(
@@ -234,16 +233,6 @@ def tile_list_airway_series_conductance_kernel(
                 )
             nc.scalar.activation(out=rb[b][:, t, :], in_=acc[:], func=ACT.Exp, scale=-1.0)
 
-        idle = bank([P, BANK], 7)
-        for t in range(HEAD_WARM):
-            nc.tensor.matmul_mx(
-                out=idle[:],
-                lhsT=wa_raw[0][:, 0, P // 2 * t : P // 2 * (t + 1)].bitcast(FP4X4),
-                lhsT_scale=wa_s_raw[:, 0, P * t : P * (t + 1)],
-                rhs=v_w[0][:, 0:BANK].bitcast(FP8X4),
-                rhs_scale=wa_s_raw[:, 0, 0:BANK],
-                start=True, stop=True,
-            )
         pieces = [(b, t, c0, c1) for b, chunks in enumerate((first_chunks, later_chunks))
                   for c0, c1 in chunks for t in range(PACK)]
         for n, piece in enumerate(pieces):

@@ -189,17 +189,27 @@ def tile_list_airway_series_conductance_kernel(
         wb_q = {(0, 0): quantize("wb_q00", first[:], KP, "tab2_w1")}
         for a, b in ((1, 0), (0, 1)):
             wb_q[a, b] = quantize("wb_q%d%d" % (a, b), cast_wb(a, b, nc.vector.tensor_copy)[:], KP)
-        last_bf = sb("wb_bf11", [P, KP * PACK], BF16)
+        last_bf = []
         for half, engine_copy in enumerate((nc.scalar.copy, nc.vector.tensor_copy)):
+            last_bf.append(sb("wb_bf11_%d" % half, [P, 2 * KP], BF16))
             engine_copy(
-                out=last_bf[:].rearrange("p (t m j) -> p m j t", t=PACK, j=PACK)[:, 64 * half : 64 * (half + 1)],
+                out=last_bf[half][:].rearrange("p (t m j) -> p m j t", t=PACK, j=PACK),
                 in_=last_raw[half][:].rearrange("p j (m t) -> p m j t", t=PACK),
             )
-        last_q = [quantize("wb_q11_%d" % pair, last_bf[:, 2 * KP * pair : 2 * KP * (pair + 1)], KP // 2)
-                  for pair in range(2)]
+        wb_q[1, 1] = sb("wb_q11_w", [P, KP], U32), sb("wb_q11_s", [P, KP], U8)
+        for half in (1, 0):
+            for t in range(PACK):
+                cols = slice(P * t + 64 * half, P * t + 64 * (half + 1))
+                nc.vector.quantize_mx(
+                    out=wb_q[1, 1][0][:, cols].bitcast(FP8X4), scales=wb_q[1, 1][1][:, cols],
+                    in_=last_bf[half][:, 2 * P * t : 2 * P * (t + 1)])
 
         ra = {(b, t): sb("ra%d%d" % (b, t), [P, S], F32) for b in range(2) for t in range(PACK)}
-        rb = [sb("rb_%d" % b, [P, PACK, M], F32, tag) for b, tag in enumerate(("wb_raw11_0", ""))]
+        rb_first = sb("rb_first", [P, M], F32)
+        rb_rest = sb("rb_rest", [P, PACK - 1, M], F32, "wb_raw11_0")
+        rb_last = sb("rb_last", [P, PACK, M], F32)
+        rb = [[rb_first[:]] + [rb_rest[:, t, :] for t in range(PACK - 1)],
+              [rb_last[:, t, :] for t in range(PACK)]]
 
         def make_ra(b, t, c0, c1, index):
             acc = bank([P, c1 - c0], index)
@@ -218,11 +228,7 @@ def tile_list_airway_series_conductance_kernel(
             acc = bank([P, BANK], index)
             cols = slice(P * t, P * (t + 1))
             for a in range(2):
-                if (a, b) == (1, 1):
-                    codes, scales = last_q[t // 2]
-                    cols = slice(P * (t % 2), P * (t % 2 + 1))
-                else:
-                    codes, scales = wb_q[a, b]
+                codes, scales = wb_q[a, b]
                 nc.tensor.matmul_mx(
                     out=acc[:],
                     lhsT=codes[:, cols].bitcast(FP8X4),
@@ -231,7 +237,7 @@ def tile_list_airway_series_conductance_kernel(
                     rhs_scale=v2_s[4:P, a, :],
                     start=(a == 0), stop=(a == 1),
                 )
-            nc.scalar.activation(out=rb[b][:, t, :], in_=acc[:], func=ACT.Exp, scale=-1.0)
+            nc.scalar.activation(out=rb[b][t], in_=acc[:], func=ACT.Exp, scale=-1.0)
 
         pieces = [(b, t, c0, c1) for b, chunks in enumerate((first_chunks, later_chunks))
                   for c0, c1 in chunks for t in range(PACK)]
@@ -241,7 +247,7 @@ def tile_list_airway_series_conductance_kernel(
             for t in range(PACK):
                 make_rb(b, t, (len(pieces) + PACK * b + t) % FIRST_BANKS)
 
-        inv_drive = sb("inv_drive", [P, 2 * PACK], F32, "wb_q11_1_s")
+        inv_drive = sb("inv_drive", [P, 2 * PACK], F32, "wb_q11_s")
         nc.vector.reciprocal(out=inv_drive[:], in_=drive_t[:].rearrange("p b t -> p (b t)"))
 
         def make_series(b, c0, width, tag=""):
@@ -250,7 +256,7 @@ def tile_list_airway_series_conductance_kernel(
                 nc.vector.tensor_tensor(
                     out=tile[:, t, :],
                     in0=ra[b, t][:].indirect(pos_t[:, c0 // 16 : (c0 + width) // 16]),
-                    in1=rb[b][:, t, c0 : c0 + width],
+                    in1=rb[b][t][:, c0 : c0 + width],
                     op=ALU.add,
                 )
             return tile
@@ -276,7 +282,7 @@ def tile_list_airway_series_conductance_kernel(
                 nc.scalar.activation(out=dst, in_=src, func=ACT.Square)
             return quantize("z_q%d_%d" % (b, c0), z_bf[:], width)
 
-        series0 = make_series(0, 0, M, "wb_raw11_1")
+        series0 = make_series(0, 0, M, "wb_bf11_0")
         series = {(0, h): series0[:, :, HALF * h : HALF * (h + 1)] for h in range(2)}
         for h in range(2):
             series[1, h] = make_series(1, HALF * h, HALF)[:]

@@ -316,7 +316,7 @@ def tile_list_airway_series_conductance_kernel(
         for h, accs in enumerate(results):
             for pair in range(2):
                 res = sb("res%d%d" % (h, pair), [P, 2, HALF], F32)
-                copies = (nc.vector.tensor_copy, nc.scalar.copy)
+                copies = (nc.vector.tensor_copy if h else nc.scalar.copy, nc.scalar.copy)
                 rows = out[2 * P * pair : 2 * P * (pair + 1), HALF * h : HALF * (h + 1)]
                 rows = rows.rearrange("(j p) m -> p j m", p=P)
                 for i, engine_copy in enumerate(copies):

from contextlib import ExitStack

import concourse.mybir as mybir

K, T, S, H, T2, M, N = 1024, 2048, 1024, 1024, 1024, 512, 512
FLOPS = 2 * K * H * S + 2 * K * H * M + 2 * H * N * M

F32 = mybir.dt.float32
BF16 = mybir.dt.bfloat16
I32 = mybir.dt.int32
U32 = mybir.dt.uint32
U16 = mybir.dt.uint16
U8 = mybir.dt.uint8
FP8X4 = mybir.dt.float8_e4m3fn_x4
FP4X4 = mybir.dt.float4_e2m1fn_x4
ACT = mybir.ActivationFunctionType
ALU = mybir.AluOpType

P = 128
PACK = 4
KP = P * PACK
BANK = 512
HALF = M // 2
FIRST_BANKS = 6


def tile_list_airway_series_conductance_kernel(
    tc, tab_words, tab_scales, tab2_words, tab2_scales, wa_words, wa_scales, wb,
    wf_words, wf_scales, drive, offs, pos1, offs2, out,
):
    nc = tc.nc
    with ExitStack() as ctx:
        keep = ctx.enter_context(tc.tile_pool(name="keep", bufs=1))
        psum = ctx.enter_context(tc.psum_pool(name="psum", bufs=1))

        def sb(name, shape, dtype, tag=""):
            return keep.tile(shape, dtype, name=name, align_bytes=64, tag=tag)

        def bank(shape, index):
            return psum.tile(shape, F32, name="bank%d" % index)

        offs_t = sb("offs_t", [P, S // 16], U16)
        pos_t = sb("pos_t", [P, M // 16], U16)
        offs2_t = sb("offs2_t", [P, M // 16], U16)

        tab_s = sb("tab_s", [P, T], U8)
        wa_s_raw = sb("wa_s_raw", [P, 2, H], U8)
        tab2_s = sb("tab2_s", [P, T2], U8)
        v2_s = sb("v2_s", [P, 2, M], U8)
        wf_s = sb("wf_s", [P, 2, N], U8)
        v_s = sb("v_s", [P, 2, S], U8)
        nc.gpsimd.memset(wa_s_raw[:].rearrange("p a n -> p (a n)").bitcast(I32), 0)
        nc.vector.memset(tab_s[0:96, :].bitcast(I32), 0)
        nc.vector.memset(v_s[:].rearrange("p a n -> p (a n)").bitcast(I32), 0)
        nc.vector.memset(tab2_s[0:96, :].bitcast(I32), 0)
        nc.vector.memset(v2_s[:].rearrange("p a n -> p (a n)").bitcast(I32), 0)
        nc.vector.memset(wf_s[:].rearrange("p a n -> p (a n)").bitcast(I32), 0)

        def load_side_by_side(plane, scales, first):
            for r in range(4):
                nc.sync.dma_start(
                    out=plane[first + r : P : 32, :, :].bitcast(I32),
                    in_=scales[:, r:16:4, :].rearrange("a q n -> q a n").bitcast(I32),
                )

        def load_rows(window, scales):
            nc.sync.dma_start(out=window[96:P, :].bitcast(I32),
                              in_=scales.rearrange("a q n -> q a n").bitcast(I32))

        def move_rows(plane, rows, first):
            for q in (0, 2, 1, 3):
                nc.sync.dma_start(
                    out=plane[32 * q + first : 32 * q + first + 4, :, :].rearrange("p a n -> p (a n)").bitcast(I32),
                    in_=rows[96 + 8 * q : 104 + 8 * q, :].bitcast(I32))

        def load_words(name, words):
            tile = sb(name, [P, words.shape[1]], I32)
            nc.sync.dma_start(out=tile[:], in_=words.rearrange("p n i -> p (n i)").bitcast(I32))
            return tile

        def load_both_passes(name, words, tag):
            tile = sb(name, [P, 2, words.shape[2]], I32, tag)
            nc.sync.dma_start(out=tile[:], in_=words.rearrange("a p n i -> p a (n i)").bitcast(I32))
            return tile

        def load_wb(a, b, tag=""):
            tile = sb("wb_raw%d%d" % (a, b), [P, PACK, KP], F32, tag)
            rows = wb[KP * a : KP * (a + 1), KP * b : KP * (b + 1)]
            nc.sync.dma_start(out=tile[:], in_=rows.rearrange("(p j) c -> p j c", j=PACK))
            return tile

        def load_wb_half(a, b, half):
            tile = sb("wb_raw%d%d_%d" % (a, b, half), [P, PACK, KP // 2], F32)
            c0 = KP * b + KP // 2 * half
            rows = wb[KP * a : KP * (a + 1), c0 : c0 + KP // 2]
            nc.sync.dma_start(out=tile[:], in_=rows.rearrange("(p j) c -> p j c", j=PACK))
            return tile

        def load_wa(b, tag=""):
            tile = sb("wa_raw%d" % b, [P, 2, KP // 2], I32, tag)
            cols = wa_words[:, :, 2 * KP * b : 2 * KP * (b + 1)]
            nc.sync.dma_start(out=tile[:], in_=cols.rearrange("a p n -> p a n").bitcast(I32))
            return tile

        nc.sync.dma_start(out=offs_t[:], in_=offs)
        load_rows(tab_s, tab_scales)
        tab_w = [load_words("tab_w0", tab_words[0])]
        wa_raw = [load_wa(0)]
        load_side_by_side(wa_s_raw, wa_scales, 0)
        tab_w.append(load_words("tab_w1", tab_words[1]))

        def gather(name, window, offsets, count, dtype, tag=""):
            tile = sb(name, [P, count], dtype, tag)
            nc.vector.tensor_copy(out=tile[:], in_=window.indirect(offsets))
            return tile

        def deal_wa(b, engine_copy):
            tile = sb("wa_w%d" % b, [P, 2, 2 * KP], U8)
            engine_copy(
                out=tile[:].rearrange("p a n -> p (a n)").bitcast(U16).rearrange(
                    "p (a t c i) -> p a c t i", t=PACK, c=16, i=8),
                in_=wa_raw[b][:].rearrange("p a n -> p (a n)").bitcast(U16).rearrange(
                    "p (a c i t) -> p a c t i", t=PACK, c=16, i=8),
            )
            return tile

        wa_w = [deal_wa(0, nc.scalar.copy)]
        v_s0 = gather("v_s0", tab_s[:], offs_t[:], S, U8)
        move_rows(v_s, v_s0, 0)
        wa_raw.append(load_wa(1, "late"))
        wb_raw = {(0, 0): load_wb(0, 0)}
        load_rows(tab2_s, tab2_scales)
        nc.sync.dma_start(out=offs2_t[:], in_=offs2)
        tab2_w = [load_words("tab2_w%d" % a, tab2_words[a]) for a in range(2)]
        wb_raw[1, 0] = load_wb(1, 0)

        v_w = [sb("v_w%d" % a, [P, S], U32) for a in range(2)]

        def gather_tab(a, c0, c1):
            nc.vector.tensor_copy(out=v_w[a][:, c0:c1],
                                  in_=tab_w[a][:].bitcast(U32).indirect(offs_t[:, c0 // 16 : c1 // 16]))

        first_chunks = ((0, 256), (256, 512), (512, 1024))
        later_chunks = ((0, 512), (512, 1024))
        wa_s = []
        for b in range(2):
            wa_s.append(sb("wa_s%d" % b, [P, 2, KP], U8))
            nc.gpsimd.tensor_copy(
                out=wa_s[b][:].rearrange("p a (t m) -> p a t m", t=PACK),
                in_=wa_s_raw[:, :, KP * b : KP * (b + 1)].rearrange("p a (m t) -> p a t m", t=PACK),
            )
        for c0, c1 in later_chunks:
            gather_tab(0, c0, c1)
        for c0, c1 in first_chunks:
            gather_tab(1, c0, c1)
        wa_w.append(deal_wa(1, nc.vector.tensor_copy))
        v2_s0 = gather("v2_s0", tab2_s[:], offs2_t[:], M, U8)
        move_rows(v2_s, v2_s0, 4)
        wb_raw[0, 1] = load_wb(0, 1)
        last_raw = [load_wb_half(1, 1, half) for half in range(2)]
        nc.sync.dma_start(out=pos_t[:], in_=pos1)
        drive_t = sb("drive_t", [P, 2, PACK], F32)
        nc.sync.dma_start(out=drive_t[:], in_=drive.rearrange("(b p t) -> p b t", p=P, t=PACK))
        wf_w = load_both_passes("wf_w", wf_words, "")
        load_side_by_side(wf_s, wf_scales, 8)

        def quantize(name, src, words, tag=""):
            codes = sb(name + "_w", [P, words], U32, tag)
            scales = sb(name + "_s", [P, words], U8)
            nc.vector.quantize_mx(out=codes[:].bitcast(FP8X4), scales=scales[:], in_=src)
            return codes, scales

        def cast_wb(a, b, engine_copy, tag=""):
            tile = sb("wb_bf%d%d" % (a, b), [P, KP * PACK], BF16, tag)
            engine_copy(
                out=tile[:].rearrange("p (t m j) -> p m j t", t=PACK, j=PACK),
                in_=wb_raw[a, b][:].rearrange("p j (m t) -> p m j t", t=PACK),
            )
            return tile

        def pool_copy(out, in_):
            for half in range(2):
                rows = slice(64 * half, 64 * (half + 1))
                nc.gpsimd.tensor_copy(out=out[:, rows].rearrange("p m j t -> p m t j"),
                                      in_=in_[:, rows].rearrange("p m j t -> p m t j"))

        first = cast_wb(0, 0, pool_copy, "late")
        v2_w = [gather("v2_w%d" % a, tab2_w[a][:].bitcast(U32), offs2_t[:], M, U32) for a in range(2)]
        wb_q = {(0, 0): quantize("wb_q00", first[:], KP, "tab2_w1")}
        for a, b in ((1, 0), (0, 1)):
            wb_q[a, b] = quantize("wb_q%d%d" % (a, b), cast_wb(a, b, nc.vector.tensor_copy)[:], KP)
        last_bf = []
        for half, engine_copy in enumerate((nc.scalar.copy, nc.vector.tensor_copy)):
            last_bf.append(sb("wb_bf11_%d" % half, [P, 2 * KP], BF16))
            engine_copy(
                out=last_bf[half][:].rearrange("p (t m j) -> p m j t", t=PACK, j=PACK),
                in_=last_raw[half][:].rearrange("p j (m t) -> p m j t", t=PACK),
            )
        wb_q[1, 1] = sb("wb_q11_w", [P, KP], U32), sb("wb_q11_s", [P, KP], U8)
        for half in (1, 0):
            for t in range(PACK):
                cols = slice(P * t + 64 * half, P * t + 64 * (half + 1))
                nc.vector.quantize_mx(
                    out=wb_q[1, 1][0][:, cols].bitcast(FP8X4), scales=wb_q[1, 1][1][:, cols],
                    in_=last_bf[half][:, 2 * P * t : 2 * P * (t + 1)])

        ra = {(b, t): sb("ra%d%d" % (b, t), [P, S], F32) for b in range(2) for t in range(PACK)}
        rb_first = sb("rb_first", [P, M], F32)
        rb_rest = sb("rb_rest", [P, PACK - 1, M], F32, "wb_raw11_0")
        rb_last = sb("rb_last", [P, PACK, M], F32)
        rb = [[rb_first[:]] + [rb_rest[:, t, :] for t in range(PACK - 1)],
              [rb_last[:, t, :] for t in range(PACK)]]

        def make_ra(b, t, c0, c1, index):
            acc = bank([P, c1 - c0], index)
            for a in range(2):
                nc.tensor.matmul_mx(
                    out=acc[:],
                    lhsT=wa_w[b][:, a, 2 * P * t : 2 * P * (t + 1)].bitcast(FP4X4),
                    lhsT_scale=wa_s[b][:, a, P * t : P * (t + 1)],
                    rhs=v_w[a][:, c0:c1].bitcast(FP8X4),
                    rhs_scale=v_s[:, a, c0:c1],
                    start=(a == 0), stop=(a == 1),
                )
            nc.scalar.activation(out=ra[b, t][:, c0:c1], in_=acc[:], func=ACT.Exp, scale=-1.0)

        def make_rb(b, t, index):
            acc = bank([P, BANK], index)
            cols = slice(P * t, P * (t + 1))
            for a in range(2):
                codes, scales = wb_q[a, b]
                nc.tensor.matmul_mx(
                    out=acc[:],
                    lhsT=codes[:, cols].bitcast(FP8X4),
                    lhsT_scale=scales[:, cols],
                    rhs=v2_w[a][:].bitcast(FP8X4),
                    rhs_scale=v2_s[4:P, a, :],
                    start=(a == 0), stop=(a == 1),
                )
            nc.scalar.activation(out=rb[b][t], in_=acc[:], func=ACT.Exp, scale=-1.0)

        pieces = [(b, t, c0, c1) for b, chunks in enumerate((first_chunks, later_chunks))
                  for c0, c1 in chunks for t in range(PACK)]
        for n, piece in enumerate(pieces):
            make_ra(*piece, n % FIRST_BANKS)
        for b in range(2):
            for t in range(PACK):
                make_rb(b, t, (len(pieces) + PACK * b + t) % FIRST_BANKS)

        inv_drive = sb("inv_drive", [P, 2 * PACK], F32, "wb_q11_s")
        nc.vector.reciprocal(out=inv_drive[:], in_=drive_t[:].rearrange("p b t -> p (b t)"))

        def make_series(b, c0, width, tag=""):
            tile = sb("series%d_%d" % (b, c0), [P, PACK, width], F32, tag)
            for t in range(PACK):
                nc.vector.tensor_tensor(
                    out=tile[:, t, :],
                    in0=ra[b, t][:].indirect(pos_t[:, c0 // 16 : (c0 + width) // 16]),
                    in1=rb[b][t][:, c0 : c0 + width],
                    op=ALU.add,
                )
            return tile

        def make_root(b, c0, series, tag=""):
            root = sb("root%d_%d" % (b, c0), [P, PACK, HALF], F32, tag)
            for t in range(PACK):
                s = PACK * b + t
                nc.scalar.activation(
                    out=root[:, t, :], in_=series[:, t, :],
                    func=ACT.Abs_reciprocal_sqrt, scale=inv_drive[:, s : s + 1],
                )
            return root

        def make_z(b, c0, root, on_vector):
            width = root.shape[2]
            z_bf = sb("z_bf%d_%d" % (b, c0), [P, width * PACK], BF16)
            dst = z_bf[:].rearrange("p (c i t) -> p c t i", i=4, t=PACK)
            src = root[:].rearrange("p t (c i) -> p c t i", i=4)
            if on_vector:
                nc.vector.tensor_tensor(out=dst, in0=src, in1=src, op=ALU.mult)
            else:
                nc.scalar.activation(out=dst, in_=src, func=ACT.Square)
            return quantize("z_q%d_%d" % (b, c0), z_bf[:], width)

        series0 = make_series(0, 0, M, "wb_bf11_0")
        series = {(0, h): series0[:, :, HALF * h : HALF * (h + 1)] for h in range(2)}
        for h in range(2):
            series[1, h] = make_series(1, HALF * h, HALF)[:]
        results = []
        for h in range(2):
            accs = [bank([P, HALF], PACK * h + j) for j in range(4)]
            for b in range(2):
                codes, scales = make_z(b, h, make_root(b, h, series[b, h]), on_vector=(b != h))
                for j in range(4):
                    ncols = slice(P * j, P * (j + 1))
                    nc.tensor.matmul_mx(
                        out=accs[j][:],
                        lhsT=wf_w[:, b, ncols].bitcast(FP8X4),
                        lhsT_scale=wf_s[8:P, b, ncols],
                        rhs=codes[:].bitcast(FP8X4),
                        rhs_scale=scales[:],
                        start=(b == 0), stop=(b == 1),
                    )
                if (b, h) == (0, 0):
                    idle = bank([P, HALF], 7)
                    for j in (0, 1, 2, 3, 0):
                        nc.tensor.matmul_mx(
                            out=idle[:],
                            lhsT=wf_w[:, 0, P * j : P * (j + 1)].bitcast(FP8X4),
                            lhsT_scale=wf_s[8:P, 0, P * j : P * (j + 1)],
                            rhs=codes[:].bitcast(FP8X4),
                            rhs_scale=scales[:],
                            start=True, stop=True,
                        )
            results.append(accs)
        for h, accs in enumerate(results):
            for pair in range(2):
                res = sb("res%d%d" % (h, pair), [P, 2, HALF], F32)
                copies = (nc.vector.tensor_copy if h else nc.scalar.copy, nc.scalar.copy)
                rows = out[2 * P * pair : 2 * P * (pair + 1), HALF * h : HALF * (h + 1)]
                rows = rows.rearrange("(j p) m -> p j m", p=P)
                for i, engine_copy in enumerate(copies):
                    engine_copy(out=res[:, i, :], in_=accs[2 * pair + i][:])
                    if h == 1:
                        nc.sync.dma_start(out=rows[:, i, :], in_=res[:, i, :])
                if h == 0:
                    nc.sync.dma_start(out=rows, in_=res[:])
